import numpy as np
import ml_dtypes


def mxq(x, axis, fmt="e4m3"):
    dtype, down = {"e4m3": (ml_dtypes.float8_e4m3fn, 7), "e5m2": (ml_dtypes.float8_e5m2, 14)}[fmt]
    v = np.moveaxis(np.asarray(x, np.float32).astype(ml_dtypes.bfloat16).astype(np.float64), axis, -1)
    blocks = v.reshape(v.shape[:-1] + (-1, 32))
    amax = np.abs(blocks).max(-1, keepdims=True)
    byte = np.maximum(np.where(amax > 0, np.frexp(amax)[1] - 1 + 127, 0) - down, 1)
    scale = np.exp2(byte - 127.0)
    codes = (blocks / scale).astype(np.float32).astype(dtype).astype(np.float64)
    return np.moveaxis((codes * scale).reshape(v.shape), -1, axis)


WIDE = False


def mx_kscale(k):
    if not WIDE:
        return np.ones(k)
    levels = np.array([10, -10, 5, -5, 0])
    if k % 512:
        return np.exp2(np.random.permutation(np.resize(levels, k // 32))).repeat(32)
    a = np.empty((k // 512, 16))
    for p in range(k // 512):
        a[p, :8] = np.random.permutation(np.resize(levels, 8))
        for g in range(8):
            far = levels[np.abs(levels - a[p, g]) >= 10]
            a[p, g + 8] = far[np.random.randint(len(far))]
    return np.exp2(a.ravel()).repeat(32)


def f64(x):
    return np.asarray(x).astype(np.float64)


def striped(idx):
    return np.tile(idx.reshape(-1, 16).T, (8, 1)).astype(np.uint16)


def unstriped(offs):
    return offs[:16].T.reshape(-1).astype(np.int64)


E2M1 = np.array([0.0, 0.5, 1.0, 1.5, 2.0, 3.0, 4.0, 6.0, -0.0, -0.5, -1.0, -1.5, -2.0, -3.0, -4.0, -6.0])


def pack_fp4(w):
    k, n = w.shape
    w = f64(np.asarray(w, np.float32).astype(ml_dtypes.bfloat16)).reshape(k // 32, 32, n)
    amax = np.abs(w).max(1)
    mant, ex = np.frexp(amax / 6.0)
    byte = np.clip(np.where(amax > 0, np.where(mant > 0.5, ex, ex - 1) + 127, 1), 1, 254)
    scaled = (w * np.exp2(127.0 - byte)[:, None, :]).reshape(k, n).astype(np.float32)
    c = np.ascontiguousarray(scaled.reshape(k // 512, 128, 4, n).transpose(0, 1, 3, 2)).astype(ml_dtypes.float4_e2m1fn).view(np.uint8) & 0xF
    words = (c[..., 0::2] | (c[..., 1::2] << 4)).reshape(k // 512, 128, 2 * n)
    return np.ascontiguousarray(words), np.ascontiguousarray(byte.astype(np.uint8).reshape(k // 512, 16, n))


def unpack_fp4(words, scales):
    g, _, n = scales.shape
    words = np.ascontiguousarray(words).reshape(g, 128, n, 2)
    nib = np.empty((g, 128, n, 4), np.uint8)
    nib[..., 0::2] = words & 0xF
    nib[..., 1::2] = words >> 4
    vals = E2M1[nib] * np.repeat(np.exp2(scales.astype(np.float64) - 127.0), 8, axis=1)[..., None]
    return vals.transpose(0, 1, 3, 2).reshape(g * 512, n)


def gelu(v):
    return 0.5 * v * (1.0 + np.tanh(np.sqrt(2.0 / np.pi) * (v + 0.044715 * v**3)))


K, T, S, H, N, U = 512, 2048, 512, 512, 256, 1024


def setup_inputs():
    n = np.random.standard_normal
    s = mx_kscale(K)[:, None]
    u = mx_kscale(H)
    packed_w2 = pack_fp4(n((H, N)) / np.sqrt(H) / u[:, None])
    return {
        "xT": (n((K, T)) * s).astype(np.float32),
        "w1": (n((K, H)) / np.sqrt(K) / s * u).astype(np.float32),
        "w2_words": packed_w2[0],
        "w2_scales": packed_w2[1],
        "skip": (n((H, U)) * u[:, None]).astype(np.float32),
        "offs": striped(np.random.permutation(T)[:S]),
        "cell": striped(np.random.permutation(U)[:S]),
    }


def reference(xT, w1, w2_words, w2_scales, skip, offs, cell):
    xq = mxq(f64(xT)[:, unstriped(offs)], 0, "e4m3")
    up = np.zeros((H, U))
    up[:, unstriped(cell)] = gelu(mxq(f64(w1), 0, "e4m3").T @ xq)
    z = up + f64(skip)
    return unpack_fp4(w2_words, w2_scales).T @ mxq(z, 0, "e4m3")

@@ -1,0 +1,154 @@
+from contextlib import ExitStack
+
+import concourse.mybir as mybir
+
+K, T, S, H, N, U = 512, 2048, 512, 512, 256, 1024
+FLOPS = 2 * K * H * S + 2 * H * N * U
+
+F32 = mybir.dt.float32
+BF16 = mybir.dt.bfloat16
+I32 = mybir.dt.int32
+U32 = mybir.dt.uint32
+U16 = mybir.dt.uint16
+U8 = mybir.dt.uint8
+FP8X4 = mybir.dt.float8_e4m3fn_x4
+FP4X4 = mybir.dt.float4_e2m1fn_x4
+ADD = mybir.AluOpType.add
+GELU = mybir.ActivationFunctionType.Gelu_apprx_tanh
+
+P = 128
+PACK = 4
+LIST_ROWS = 16
+HALF = S // 2
+CHUNK = 256
+
+
+def tile_picked_unet_gelu_e_kernel(tc, xT, w1, w2_words, w2_scales, skip, offs, cell, out):
+    nc = tc.nc
+    with ExitStack() as ctx:
+        keep = ctx.enter_context(tc.tile_pool(name="keep", bufs=1))
+        psum = ctx.enter_context(tc.psum_pool(name="psum", bufs=4))
+
+        offs_sb = keep.tile([P, S // LIST_ROWS], U16, name="offs_sb")
+        cell_sb = keep.tile([P, S // LIST_ROWS], U16, name="cell_sb")
+        w1_raw = keep.tile([P, PACK, H], F32, name="w1_raw")
+        x_rows = [keep.tile([P, T], F32, name=f"x_rows{j}") for j in range(PACK)]
+        skip_rows = [keep.tile([P, U], F32, name=f"skip_rows{t}") for t in range(PACK)]
+        up = [keep.tile([P, U], F32, name=f"up{t}") for t in range(PACK)]
+        w2_codes = keep.tile([P, 2 * N], U8, name="w2_codes", align_bytes=64)
+        w2_scale = keep.tile([P, N], U8, name="w2_scale", align_bytes=64)
+
+        nc.vector.memset(w2_scale[:].bitcast(I32), 0)
+        for t in range(PACK):
+            nc.vector.memset(up[t][:], 0.0)
+
+        x_planes = xT.rearrange("(p j) c -> p j c", j=PACK)
+        skip_planes = skip.rearrange("(p t) v -> p t v", t=PACK)
+        nc.sync.dma_start(out=w1_raw[:], in_=w1.rearrange("(p j) c -> p j c", j=PACK))
+        nc.sync.dma_start(offs_sb[:], offs)
+        for j in range(PACK):
+            nc.sync.dma_start(out=x_rows[j][:], in_=x_planes[:, j, :])
+        nc.sync.dma_start(cell_sb[:], cell)
+        for t in range(PACK):
+            nc.sync.dma_start(out=skip_rows[t][:], in_=skip_planes[:, t, :])
+        nc.sync.dma_start(out=w2_codes[:].bitcast(I32), in_=w2_words[0].bitcast(I32))
+        for q in range(4):
+            nc.sync.dma_start(
+                out=w2_scale[32 * q : 32 * q + 4, :].bitcast(I32),
+                in_=w2_scales[0, 4 * q : 4 * q + 4, :].bitcast(I32),
+            )
+
+        w1_grouped = keep.tile([P, PACK, P, PACK], BF16, name="w1_grouped", align_bytes=64)
+        w1_codes = keep.tile([P, H], U32, name="w1_codes", align_bytes=64)
+        w1_scale = keep.tile([P, H], U8, name="w1_scale", align_bytes=64)
+        nc.vector.tensor_copy(
+            out=w1_grouped[:].rearrange("p t m j -> p m j t"),
+            in_=w1_raw[:].rearrange("p j (m t) -> p m j t", t=PACK),
+        )
+        nc.vector.quantize_mx(
+            out=w1_codes[:].bitcast(FP8X4),
+            scales=w1_scale[:],
+            in_=w1_grouped[:].rearrange("p t m j -> p (t m j)"),
+        )
+
+        x_grouped = keep.tile([P, S, PACK], BF16, name="x_grouped", align_bytes=64)
+        x_codes = keep.tile([P, S], U32, name="x_codes", align_bytes=64)
+        x_scale = keep.tile([P, S], U8, name="x_scale", align_bytes=64)
+        for j in range(PACK - 1):
+            nc.vector.tensor_copy(x_grouped[:, :, j], x_rows[j][:].indirect(offs_sb[:]))
+        halves = [slice(0, HALF), slice(HALF, S)]
+        lists = [slice(0, HALF // LIST_ROWS), slice(HALF // LIST_ROWS, S // LIST_ROWS)]
+        for entries, cols in zip(halves, lists):
+            nc.vector.tensor_copy(x_grouped[:, entries, PACK - 1], x_rows[PACK - 1][:].indirect(offs_sb[:, cols]))
+            nc.vector.quantize_mx(
+                out=x_codes[:, entries].bitcast(FP8X4),
+                scales=x_scale[:, entries],
+                in_=x_grouped[:, entries, :].rearrange("p s j -> p (s j)"),
+            )
+
+        def first_layer(t, entries, cols):
+            width = entries.stop - entries.start
+            channels = slice(t * P, (t + 1) * P)
+            pre = psum.tile([P, width], F32, name="pre")
+            nc.tensor.matmul_mx(
+                out=pre[:],
+                lhsT=w1_codes[:, channels].bitcast(FP8X4),
+                lhsT_scale=w1_scale[:, channels],
+                rhs=x_codes[:, entries].bitcast(FP8X4),
+                rhs_scale=x_scale[:, entries],
+                start=True,
+                stop=True,
+            )
+            h = keep.tile([P, width], F32, name=f"h{t}_{entries.start}")
+            nc.scalar.activation(h[:], pre[:], GELU)
+            nc.vector.tensor_copy(up[t][:].indirect(cell_sb[:, cols]), h[:])
+
+        z_planes = keep.tile([P, PACK, U], BF16, name="z_planes")
+        z_grouped = keep.tile([P, U, PACK], BF16, name="z_grouped", align_bytes=64)
+        for entries, cols in zip(halves, lists):
+            first_layer(0, entries, cols)
+        for t in range(1, PACK):
+            first_layer(t, slice(0, S), slice(0, S // LIST_ROWS))
+        for t in range(PACK - 1):
+            nc.gpsimd.tensor_tensor(z_planes[:, t, :], up[t][:], skip_rows[t][:], ADD)
+        nc.scalar.copy(z_grouped[:, :, 0:2], z_planes[:, 0:2, :].rearrange("p t v -> p v t"))
+
+        z_codes = keep.tile([P, U], U32, name="z_codes", align_bytes=64)
+        z_scale = keep.tile([P, U], U8, name="z_scale", align_bytes=64)
+        out_blocks = out.rearrange("(b m) v -> m b v", m=P)
+        chunks = [slice(c, c + CHUNK) for c in range(0, U, CHUNK)]
+
+        def add_last(cells):
+            nc.vector.tensor_tensor(z_planes[:, PACK - 1, cells], up[PACK - 1][:, cells], skip_rows[PACK - 1][:, cells], ADD)
+
+        def weave(cells):
+            nc.vector.tensor_copy(z_grouped[:, cells, 2:4], z_planes[:, 2:4, cells].rearrange("p t v -> p v t"))
+
+        def second_layer(cells):
+            nc.vector.quantize_mx(
+                out=z_codes[:, cells].bitcast(FP8X4),
+                scales=z_scale[:, cells],
+                in_=z_grouped[:, cells, :].rearrange("p v t -> p (v t)"),
+            )
+            acc = psum.tile([P, N // P, CHUNK], F32, name="acc")
+            for b in range(N // P):
+                nc.tensor.matmul_mx(
+                    out=acc[:, b, :],
+                    lhsT=w2_codes[:, 2 * P * b : 2 * P * (b + 1)].bitcast(FP4X4),
+                    lhsT_scale=w2_scale[:, P * b : P * (b + 1)],
+                    rhs=z_codes[:, cells].bitcast(FP8X4),
+                    rhs_scale=z_scale[:, cells],
+                    start=True,
+                    stop=True,
+                )
+            result = keep.tile([P, N // P, CHUNK], F32, name=f"result{cells.start}")
+            nc.scalar.copy(result[:], acc[:])
+            nc.sync.dma_start(out=out_blocks[:, :, cells], in_=result[:])
+
+        for step in range(len(chunks) + 2):
+            if step < len(chunks):
+                add_last(chunks[step])
+            if 1 <= step <= len(chunks):
+                weave(chunks[step - 1])
+            if step >= 2:
+                second_layer(chunks[step - 2])

@@ -31,7 +31,7 @@ def tile_picked_unet_gelu_e_kernel(tc, xT, w1, w2_words, w2_scales, skip, offs, 
 
         offs_sb = keep.tile([P, S // LIST_ROWS], U16, name="offs_sb")
         cell_sb = keep.tile([P, S // LIST_ROWS], U16, name="cell_sb")
-        w1_raw = keep.tile([P, PACK, H], F32, name="w1_raw")
+        w1_raw = [keep.tile([P, PACK, H // 2], F32, name=f"w1_raw{a}") for a in range(2)]
         x_rows = [keep.tile([P, T], F32, name=f"x_rows{j}") for j in range(PACK)]
         skip_rows = [keep.tile([P, U], F32, name=f"skip_rows{t}") for t in range(PACK)]
         up = [keep.tile([P, U], F32, name=f"up{t}") for t in range(PACK)]
@@ -42,12 +42,18 @@ def tile_picked_unet_gelu_e_kernel(tc, xT, w1, w2_words, w2_scales, skip, offs, 
         for t in range(PACK):
             nc.vector.memset(up[t][:], 0.0)
 
+        warm = keep.tile([P, 1], F32, name="warm")
+        nc.scalar.activation(warm[:], up[0][:, 0:1], GELU)
+
         x_planes = xT.rearrange("(p j) c -> p j c", j=PACK)
         skip_planes = skip.rearrange("(p t) v -> p t v", t=PACK)
-        nc.sync.dma_start(out=w1_raw[:], in_=w1.rearrange("(p j) c -> p j c", j=PACK))
-        nc.sync.dma_start(offs_sb[:], offs)
+        w1_planes = w1.rearrange("(p j) c -> p j c", j=PACK)
         for j in range(PACK):
             nc.sync.dma_start(out=x_rows[j][:], in_=x_planes[:, j, :])
+            if j == 0:
+                nc.sync.dma_start(offs_sb[:], offs)
+        for a in range(2):
+            nc.sync.dma_start(out=w1_raw[a][:], in_=w1_planes[:, :, a * H // 2 : (a + 1) * H // 2])
         nc.sync.dma_start(cell_sb[:], cell)
         for t in range(PACK):
             nc.sync.dma_start(out=skip_rows[t][:], in_=skip_planes[:, t, :])
@@ -61,15 +67,6 @@ def tile_picked_unet_gelu_e_kernel(tc, xT, w1, w2_words, w2_scales, skip, offs, 
         w1_grouped = keep.tile([P, PACK, P, PACK], BF16, name="w1_grouped", align_bytes=64)
         w1_codes = keep.tile([P, H], U32, name="w1_codes", align_bytes=64)
         w1_scale = keep.tile([P, H], U8, name="w1_scale", align_bytes=64)
-        nc.vector.tensor_copy(
-            out=w1_grouped[:].rearrange("p t m j -> p m j t"),
-            in_=w1_raw[:].rearrange("p j (m t) -> p m j t", t=PACK),
-        )
-        nc.vector.quantize_mx(
-            out=w1_codes[:].bitcast(FP8X4),
-            scales=w1_scale[:],
-            in_=w1_grouped[:].rearrange("p t m j -> p (t m j)"),
-        )
 
         x_grouped = keep.tile([P, S, PACK], BF16, name="x_grouped", align_bytes=64)
         x_codes = keep.tile([P, S], U32, name="x_codes", align_bytes=64)
@@ -85,6 +82,27 @@ def tile_picked_unet_gelu_e_kernel(tc, xT, w1, w2_words, w2_scales, skip, offs, 
                 scales=x_scale[:, entries],
                 in_=x_grouped[:, entries, :].rearrange("p s j -> p (s j)"),
             )
+
+        def group_w1(copy, a, tiles):
+            copy(
+                w1_grouped[:, tiles, a * P // 2 : (a + 1) * P // 2, :].rearrange("p t m j -> p m j t"),
+                w1_raw[a][:].rearrange("p j (m t) -> p m j t", t=PACK)[:, :, :, tiles],
+            )
+
+        def quantize_w1(tiles):
+            channels = slice(tiles.start * P, tiles.stop * P)
+            nc.vector.quantize_mx(
+                out=w1_codes[:, channels].bitcast(FP8X4),
+                scales=w1_scale[:, channels],
+                in_=w1_grouped[:, tiles, :, :].rearrange("p t m j -> p (t m j)"),
+            )
+
+        group_w1(nc.scalar.copy, 0, slice(0, PACK))
+        group_w1(nc.vector.tensor_copy, 1, slice(0, 1))
+        quantize_w1(slice(0, 1))
+        group_w1(nc.vector.tensor_copy, 1, slice(1, PACK))
+        quantize_w1(slice(1, 2))
+        quantize_w1(slice(2, PACK))
 
         def first_layer(t, entries, cols):
             width = entries.stop - entries.start
@@ -121,8 +139,8 @@ def tile_picked_unet_gelu_e_kernel(tc, xT, w1, w2_words, w2_scales, skip, offs, 
         def add_last(cells):
             nc.vector.tensor_tensor(z_planes[:, PACK - 1, cells], up[PACK - 1][:, cells], skip_rows[PACK - 1][:, cells], ADD)
 
-        def weave(cells):
-            nc.vector.tensor_copy(z_grouped[:, cells, 2:4], z_planes[:, 2:4, cells].rearrange("p t v -> p v t"))
+        def weave(copy, cells):
+            copy(z_grouped[:, cells, 2:4], z_planes[:, 2:4, cells].rearrange("p t v -> p v t"))
 
         def second_layer(cells):
             nc.vector.quantize_mx(
@@ -141,14 +159,26 @@ def tile_picked_unet_gelu_e_kernel(tc, xT, w1, w2_words, w2_scales, skip, offs, 
                     start=True,
                     stop=True,
                 )
+            return acc
+
+        def leave(copy, acc, cells):
             result = keep.tile([P, N // P, CHUNK], F32, name=f"result{cells.start}")
-            nc.scalar.copy(result[:], acc[:])
+            copy(result[:], acc[:])
             nc.sync.dma_start(out=out_blocks[:, :, cells], in_=result[:])
 
-        for step in range(len(chunks) + 2):
-            if step < len(chunks):
-                add_last(chunks[step])
-            if 1 <= step <= len(chunks):
-                weave(chunks[step - 1])
-            if step >= 2:
-                second_layer(chunks[step - 2])
+        add_last(chunks[0])
+        add_last(chunks[1])
+        weave(nc.vector.tensor_copy, chunks[0])
+        weave(nc.scalar.copy, chunks[1])
+        add_last(chunks[2])
+        acc0 = second_layer(chunks[0])
+        weave(nc.scalar.copy, chunks[2])
+        add_last(chunks[3])
+        acc1 = second_layer(chunks[1])
+        leave(nc.scalar.copy, acc0, chunks[0])
+        weave(nc.vector.tensor_copy, chunks[3])
+        acc2 = second_layer(chunks[2])
+        leave(nc.scalar.copy, acc1, chunks[1])
+        acc3 = second_layer(chunks[3])
+        leave(nc.vector.tensor_copy, acc2, chunks[2])
+        leave(nc.scalar.copy, acc3, chunks[3])

@@ -33,7 +33,9 @@ def tile_picked_unet_gelu_e_kernel(tc, xT, w1, w2_words, w2_scales, skip, offs, 
         cell_sb = keep.tile([P, S // LIST_ROWS], U16, name="cell_sb")
         w1_raw = [keep.tile([P, PACK, H // 2], F32, name=f"w1_raw{a}") for a in range(2)]
         x_rows = [keep.tile([P, T], F32, name=f"x_rows{j}") for j in range(PACK)]
-        skip_rows = [keep.tile([P, U], F32, name=f"skip_rows{t}") for t in range(PACK)]
+        pair = keep.tile([P, U + U // 2], F32, name="pair")
+        skip_rows = [pair[:, U // 2 :] if t == 2 else keep.tile([P, U], F32, name=f"skip_rows{t}")[:] for t in range(PACK)]
+        z_high = pair[:].bitcast(BF16).rearrange("p (r v) -> p r v", v=U)
         up = [keep.tile([P, U], F32, name=f"up{t}") for t in range(PACK)]
         w2_codes = keep.tile([P, 2 * N], U8, name="w2_codes", align_bytes=64)
         w2_scale = keep.tile([P, N], U8, name="w2_scale", align_bytes=64)
@@ -56,7 +58,7 @@ def tile_picked_unet_gelu_e_kernel(tc, xT, w1, w2_words, w2_scales, skip, offs, 
             nc.sync.dma_start(out=w1_raw[a][:], in_=w1_planes[:, :, a * H // 2 : (a + 1) * H // 2])
         nc.sync.dma_start(cell_sb[:], cell)
         for t in range(PACK):
-            nc.sync.dma_start(out=skip_rows[t][:], in_=skip_planes[:, t, :])
+            nc.sync.dma_start(out=skip_rows[t], in_=skip_planes[:, t, :])
         nc.sync.dma_start(out=w2_codes[:].bitcast(I32), in_=w2_words[0].bitcast(I32))
         for q in range(4):
             nc.sync.dma_start(
@@ -121,15 +123,18 @@ def tile_picked_unet_gelu_e_kernel(tc, xT, w1, w2_words, w2_scales, skip, offs, 
             nc.scalar.activation(h[:], pre[:], GELU)
             nc.vector.tensor_copy(up[t][:].indirect(cell_sb[:, cols]), h[:])
 
-        z_planes = keep.tile([P, PACK, U], BF16, name="z_planes")
+        z_low = keep.tile([P, 2, U], BF16, name="z_low")
         z_grouped = keep.tile([P, U, PACK], BF16, name="z_grouped", align_bytes=64)
         for entries, cols in zip(halves, lists):
-            first_layer(0, entries, cols)
-        for t in range(1, PACK):
+            for t in range(2):
+                first_layer(t, entries, cols)
+        for t in range(2, PACK):
             first_layer(t, slice(0, S), slice(0, S // LIST_ROWS))
-        for t in range(PACK - 1):
-            nc.gpsimd.tensor_tensor(z_planes[:, t, :], up[t][:], skip_rows[t][:], ADD)
-        nc.scalar.copy(z_grouped[:, :, 0:2], z_planes[:, 0:2, :].rearrange("p t v -> p v t"))
+        for t in range(2):
+            nc.gpsimd.tensor_tensor(z_low[:, t, :], up[t][:], skip_rows[t], ADD)
+        nc.gpsimd.tensor_tensor(z_high[:, 0, :], up[2][:], skip_rows[2], ADD)
+        for cells in (slice(0, U // 2), slice(U // 2, U)):
+            nc.scalar.copy(z_grouped[:, cells, 0:2], z_low[:, :, cells].rearrange("p t v -> p v t"))
 
         z_codes = keep.tile([P, U], U32, name="z_codes", align_bytes=64)
         z_scale = keep.tile([P, U], U8, name="z_scale", align_bytes=64)
@@ -137,28 +142,34 @@ def tile_picked_unet_gelu_e_kernel(tc, xT, w1, w2_words, w2_scales, skip, offs, 
         chunks = [slice(c, c + CHUNK) for c in range(0, U, CHUNK)]
 
         def add_last(cells):
-            nc.vector.tensor_tensor(z_planes[:, PACK - 1, cells], up[PACK - 1][:, cells], skip_rows[PACK - 1][:, cells], ADD)
+            nc.vector.tensor_tensor(z_high[:, 1, cells], up[PACK - 1][:, cells], skip_rows[PACK - 1][:, cells], ADD)
 
         def weave(copy, cells):
-            copy(z_grouped[:, cells, 2:4], z_planes[:, 2:4, cells].rearrange("p t v -> p v t"))
+            copy(z_grouped[:, cells, 2:4], z_high[:, 0:2, cells].rearrange("p t v -> p v t"))
 
-        def second_layer(cells):
+        def quantize_z(cells):
             nc.vector.quantize_mx(
                 out=z_codes[:, cells].bitcast(FP8X4),
                 scales=z_scale[:, cells],
                 in_=z_grouped[:, cells, :].rearrange("p v t -> p (v t)"),
             )
+
+        def second_layer(acc, b, cells):
+            nc.tensor.matmul_mx(
+                out=acc,
+                lhsT=w2_codes[:, 2 * P * b : 2 * P * (b + 1)].bitcast(FP4X4),
+                lhsT_scale=w2_scale[:, P * b : P * (b + 1)],
+                rhs=z_codes[:, cells].bitcast(FP8X4),
+                rhs_scale=z_scale[:, cells],
+                start=True,
+                stop=True,
+            )
+
+        def both_blocks(cells):
+            quantize_z(cells)
             acc = psum.tile([P, N // P, CHUNK], F32, name="acc")
             for b in range(N // P):
-                nc.tensor.matmul_mx(
-                    out=acc[:, b, :],
-                    lhsT=w2_codes[:, 2 * P * b : 2 * P * (b + 1)].bitcast(FP4X4),
-                    lhsT_scale=w2_scale[:, P * b : P * (b + 1)],
-                    rhs=z_codes[:, cells].bitcast(FP8X4),
-                    rhs_scale=z_scale[:, cells],
-                    start=True,
-                    stop=True,
-                )
+                second_layer(acc[:, b, :], b, cells)
             return acc
 
         def leave(copy, acc, cells):
@@ -171,14 +182,19 @@ def tile_picked_unet_gelu_e_kernel(tc, xT, w1, w2_words, w2_scales, skip, offs, 
         weave(nc.vector.tensor_copy, chunks[0])
         weave(nc.scalar.copy, chunks[1])
         add_last(chunks[2])
-        acc0 = second_layer(chunks[0])
+        acc0 = both_blocks(chunks[0])
         weave(nc.scalar.copy, chunks[2])
         add_last(chunks[3])
-        acc1 = second_layer(chunks[1])
+        acc1 = both_blocks(chunks[1])
         leave(nc.scalar.copy, acc0, chunks[0])
         weave(nc.vector.tensor_copy, chunks[3])
-        acc2 = second_layer(chunks[2])
+        acc2 = both_blocks(chunks[2])
         leave(nc.scalar.copy, acc1, chunks[1])
-        acc3 = second_layer(chunks[3])
+        quantize_z(chunks[3])
         leave(nc.vector.tensor_copy, acc2, chunks[2])
-        leave(nc.scalar.copy, acc3, chunks[3])
+        last = keep.tile([P, N // P, CHUNK], F32, name="last")
+        for b in range(N // P):
+            acc = psum.tile([P, CHUNK], F32, name="acc")
+            second_layer(acc[:], b, chunks[3])
+            nc.scalar.copy(last[:, b, :], acc[:])
+        nc.sync.dma_start(out=out_blocks[:, :, chunks[3]], in_=last[:])

@@ -21,6 +21,7 @@ PACK = 4
 LIST_ROWS = 16
 HALF = S // 2
 CHUNK = 256
+FIRST_SHARE = 88
 
 
 def tile_picked_unet_gelu_e_kernel(tc, xT, w1, w2_words, w2_scales, skip, offs, cell, out):
@@ -31,7 +32,7 @@ def tile_picked_unet_gelu_e_kernel(tc, xT, w1, w2_words, w2_scales, skip, offs, 
 
         offs_sb = keep.tile([P, S // LIST_ROWS], U16, name="offs_sb")
         cell_sb = keep.tile([P, S // LIST_ROWS], U16, name="cell_sb")
-        w1_raw = [keep.tile([P, PACK, H // 2], F32, name=f"w1_raw{a}") for a in range(2)]
+        w1_raw = keep.tile([P, PACK, H], F32, name="w1_raw")
         x_rows = [keep.tile([P, T], F32, name=f"x_rows{j}") for j in range(PACK)]
         pair = keep.tile([P, U + U // 2], F32, name="pair")
         skip_rows = [pair[:, U // 2 :] if t == 2 else keep.tile([P, U], F32, name=f"skip_rows{t}")[:] for t in range(PACK)]
@@ -54,8 +55,7 @@ def tile_picked_unet_gelu_e_kernel(tc, xT, w1, w2_words, w2_scales, skip, offs, 
             nc.sync.dma_start(out=x_rows[j][:], in_=x_planes[:, j, :])
             if j == 0:
                 nc.sync.dma_start(offs_sb[:], offs)
-        for a in range(2):
-            nc.sync.dma_start(out=w1_raw[a][:], in_=w1_planes[:, :, a * H // 2 : (a + 1) * H // 2])
+        nc.sync.dma_start(out=w1_raw[:], in_=w1_planes)
         nc.sync.dma_start(cell_sb[:], cell)
         for t in range(PACK):
             nc.sync.dma_start(out=skip_rows[t], in_=skip_planes[:, t, :])
@@ -85,10 +85,10 @@ def tile_picked_unet_gelu_e_kernel(tc, xT, w1, w2_words, w2_scales, skip, offs, 
                 in_=x_grouped[:, entries, :].rearrange("p s j -> p (s j)"),
             )
 
-        def group_w1(copy, a, tiles):
+        def group_w1(copy, tiles, rows):
             copy(
-                w1_grouped[:, tiles, a * P // 2 : (a + 1) * P // 2, :].rearrange("p t m j -> p m j t"),
-                w1_raw[a][:].rearrange("p j (m t) -> p m j t", t=PACK)[:, :, :, tiles],
+                w1_grouped[:, tiles, rows, :].rearrange("p t m j -> p m j t"),
+                w1_raw[:].rearrange("p j (m t) -> p m j t", t=PACK)[:, rows, :, tiles],
             )
 
         def quantize_w1(tiles):
@@ -99,37 +99,43 @@ def tile_picked_unet_gelu_e_kernel(tc, xT, w1, w2_words, w2_scales, skip, offs, 
                 in_=w1_grouped[:, tiles, :, :].rearrange("p t m j -> p (t m j)"),
             )
 
-        group_w1(nc.scalar.copy, 0, slice(0, PACK))
-        group_w1(nc.vector.tensor_copy, 1, slice(0, 1))
+        low, high = slice(0, 2), slice(2, PACK)
+        group_w1(nc.vector.tensor_copy, low, slice(0, FIRST_SHARE))
+        group_w1(nc.scalar.copy, low, slice(FIRST_SHARE, P))
+        group_w1(nc.vector.tensor_copy, high, slice(0, P // 2))
+        group_w1(nc.scalar.copy, high, slice(P // 2, P))
         quantize_w1(slice(0, 1))
-        group_w1(nc.vector.tensor_copy, 1, slice(1, PACK))
         quantize_w1(slice(1, 2))
-        quantize_w1(slice(2, PACK))
+        quantize_w1(high)
 
-        def first_layer(t, entries, cols):
-            width = entries.stop - entries.start
+        def first_layer(t, bounds):
+            first, width = bounds[0], bounds[-1] - bounds[0]
+            entries = slice(bounds[0], bounds[-1])
+            cols = slice(bounds[0] // LIST_ROWS, bounds[-1] // LIST_ROWS)
             channels = slice(t * P, (t + 1) * P)
             pre = psum.tile([P, width], F32, name="pre")
-            nc.tensor.matmul_mx(
-                out=pre[:],
-                lhsT=w1_codes[:, channels].bitcast(FP8X4),
-                lhsT_scale=w1_scale[:, channels],
-                rhs=x_codes[:, entries].bitcast(FP8X4),
-                rhs_scale=x_scale[:, entries],
-                start=True,
-                stop=True,
-            )
+            for lo, hi in zip(bounds[:-1], bounds[1:]):
+                nc.tensor.matmul_mx(
+                    out=pre[:, lo - first : hi - first],
+                    lhsT=w1_codes[:, channels].bitcast(FP8X4),
+                    lhsT_scale=w1_scale[:, channels],
+                    rhs=x_codes[:, lo:hi].bitcast(FP8X4),
+                    rhs_scale=x_scale[:, lo:hi],
+                    start=True,
+                    stop=True,
+                )
             h = keep.tile([P, width], F32, name=f"h{t}_{entries.start}")
             nc.scalar.activation(h[:], pre[:], GELU)
             nc.vector.tensor_copy(up[t][:].indirect(cell_sb[:, cols]), h[:])
 
         z_low = keep.tile([P, 2, U], BF16, name="z_low")
         z_grouped = keep.tile([P, U, PACK], BF16, name="z_grouped", align_bytes=64)
-        for entries, cols in zip(halves, lists):
-            for t in range(2):
-                first_layer(t, entries, cols)
+        first_layer(0, [0, 128])
+        first_layer(1, [0, HALF])
+        first_layer(0, [128, HALF, S])
+        first_layer(1, [HALF, S])
         for t in range(2, PACK):
-            first_layer(t, slice(0, S), slice(0, S // LIST_ROWS))
+            first_layer(t, [0, S])
         for t in range(2):
             nc.gpsimd.tensor_tensor(z_low[:, t, :], up[t][:], skip_rows[t], ADD)
         nc.gpsimd.tensor_tensor(z_high[:, 0, :], up[2][:], skip_rows[2], ADD)

@@ -20,23 +20,28 @@ P = 128
 PACK = 4
 LIST_ROWS = 16
 HALF = S // 2
-CHUNK = 256
-FIRST_SHARE = 88
+CHUNK = 128
+AHEAD = 4
 
 
 def tile_picked_unet_gelu_e_kernel(tc, xT, w1, w2_words, w2_scales, skip, offs, cell, out):
     nc = tc.nc
     with ExitStack() as ctx:
         keep = ctx.enter_context(tc.tile_pool(name="keep", bufs=1))
-        psum = ctx.enter_context(tc.psum_pool(name="psum", bufs=4))
+        psum = ctx.enter_context(tc.psum_pool(name="psum", bufs=8))
 
         offs_sb = keep.tile([P, S // LIST_ROWS], U16, name="offs_sb")
         cell_sb = keep.tile([P, S // LIST_ROWS], U16, name="cell_sb")
-        w1_raw = keep.tile([P, PACK, H], F32, name="w1_raw")
+        w1_raw = [keep.tile([P, PACK, H // 2], F32, name=f"w1_raw{a}", align_bytes=64) for a in range(2)]
         x_rows = [keep.tile([P, T], F32, name=f"x_rows{j}") for j in range(PACK)]
-        pair = keep.tile([P, U + U // 2], F32, name="pair")
-        skip_rows = [pair[:, U // 2 :] if t == 2 else keep.tile([P, U], F32, name=f"skip_rows{t}")[:] for t in range(PACK)]
-        z_high = pair[:].bitcast(BF16).rearrange("p (r v) -> p r v", v=U)
+        work = keep.tile([P, U // 2 + U + 2 * U], F32, name="work", align_bytes=64)
+        skip_rows = [
+            work[:, U // 2 : U // 2 + U] if t == 2 else keep.tile([P, U], F32, name=f"skip_rows{t}")[:] for t in range(PACK)
+        ]
+        halfwords = work[:].bitcast(BF16)
+        z_third = halfwords[:, 0:U]
+        z_grouped = halfwords[:, 3 * U :].rearrange("p (v t) -> p v t", t=PACK)
+        runs = halfwords.rearrange("p (r v) -> p r v", v=CHUNK)
         up = [keep.tile([P, U], F32, name=f"up{t}") for t in range(PACK)]
         w2_codes = keep.tile([P, 2 * N], U8, name="w2_codes", align_bytes=64)
         w2_scale = keep.tile([P, N], U8, name="w2_scale", align_bytes=64)
@@ -55,7 +60,8 @@ def tile_picked_unet_gelu_e_kernel(tc, xT, w1, w2_words, w2_scales, skip, offs, 
             nc.sync.dma_start(out=x_rows[j][:], in_=x_planes[:, j, :])
             if j == 0:
                 nc.sync.dma_start(offs_sb[:], offs)
-        nc.sync.dma_start(out=w1_raw[:], in_=w1_planes)
+        for a in range(2):
+            nc.sync.dma_start(out=w1_raw[a][:], in_=w1_planes[:, :, a * H // 2 : (a + 1) * H // 2])
         nc.sync.dma_start(cell_sb[:], cell)
         for t in range(PACK):
             nc.sync.dma_start(out=skip_rows[t], in_=skip_planes[:, t, :])
@@ -71,24 +77,25 @@ def tile_picked_unet_gelu_e_kernel(tc, xT, w1, w2_words, w2_scales, skip, offs, 
         w1_scale = keep.tile([P, H], U8, name="w1_scale", align_bytes=64)
 
         x_grouped = keep.tile([P, S, PACK], BF16, name="x_grouped", align_bytes=64)
-        x_codes = keep.tile([P, S], U32, name="x_codes", align_bytes=64)
         x_scale = keep.tile([P, S], U8, name="x_scale", align_bytes=64)
         for j in range(PACK - 1):
             nc.vector.tensor_copy(x_grouped[:, :, j], x_rows[j][:].indirect(offs_sb[:]))
         halves = [slice(0, HALF), slice(HALF, S)]
-        lists = [slice(0, HALF // LIST_ROWS), slice(HALF // LIST_ROWS, S // LIST_ROWS)]
-        for entries, cols in zip(halves, lists):
+        for entries in halves:
+            cols = slice(entries.start // LIST_ROWS, entries.stop // LIST_ROWS)
             nc.vector.tensor_copy(x_grouped[:, entries, PACK - 1], x_rows[PACK - 1][:].indirect(offs_sb[:, cols]))
+
+        def quantize_x(codes, entries):
             nc.vector.quantize_mx(
-                out=x_codes[:, entries].bitcast(FP8X4),
+                out=codes[:].bitcast(FP8X4),
                 scales=x_scale[:, entries],
                 in_=x_grouped[:, entries, :].rearrange("p s j -> p (s j)"),
             )
 
-        def group_w1(copy, tiles, rows):
+        def group_w1(copy, a, tiles):
             copy(
-                w1_grouped[:, tiles, rows, :].rearrange("p t m j -> p m j t"),
-                w1_raw[:].rearrange("p j (m t) -> p m j t", t=PACK)[:, rows, :, tiles],
+                w1_grouped[:, tiles, a * P // 2 : (a + 1) * P // 2, :].rearrange("p t m j -> p m j t"),
+                w1_raw[a][:].rearrange("p j (m t) -> p m j t", t=PACK)[:, :, :, tiles],
             )
 
         def quantize_w1(tiles):
@@ -99,27 +106,32 @@ def tile_picked_unet_gelu_e_kernel(tc, xT, w1, w2_words, w2_scales, skip, offs, 
                 in_=w1_grouped[:, tiles, :, :].rearrange("p t m j -> p (t m j)"),
             )
 
+        x_front = keep.tile([P, HALF], U32, name="x_front", align_bytes=64)
+        quantize_x(x_front, halves[0])
         low, high = slice(0, 2), slice(2, PACK)
-        group_w1(nc.vector.tensor_copy, low, slice(0, FIRST_SHARE))
-        group_w1(nc.scalar.copy, low, slice(FIRST_SHARE, P))
-        group_w1(nc.vector.tensor_copy, high, slice(0, P // 2))
-        group_w1(nc.scalar.copy, high, slice(P // 2, P))
+        group_w1(nc.scalar.copy, 0, low)
+        group_w1(nc.scalar.copy, 0, high)
+        group_w1(nc.vector.tensor_copy, 1, low)
+        group_w1(nc.scalar.copy, 1, high)
         quantize_w1(slice(0, 1))
         quantize_w1(slice(1, 2))
+        x_back = keep.tile([P, HALF], U32, name="x_back", tag="w1_raw1", align_bytes=64)
+        quantize_x(x_back, halves[1])
         quantize_w1(high)
+        x_codes = [x_front, x_back]
 
         def first_layer(t, bounds):
             first, width = bounds[0], bounds[-1] - bounds[0]
             entries = slice(bounds[0], bounds[-1])
             cols = slice(bounds[0] // LIST_ROWS, bounds[-1] // LIST_ROWS)
             channels = slice(t * P, (t + 1) * P)
-            pre = psum.tile([P, width], F32, name="pre")
+            pre = psum.tile([P, width], F32, name="pre", tag="bank")
             for lo, hi in zip(bounds[:-1], bounds[1:]):
                 nc.tensor.matmul_mx(
                     out=pre[:, lo - first : hi - first],
                     lhsT=w1_codes[:, channels].bitcast(FP8X4),
                     lhsT_scale=w1_scale[:, channels],
-                    rhs=x_codes[:, lo:hi].bitcast(FP8X4),
+                    rhs=x_codes[lo // HALF][:, lo % HALF : lo % HALF + hi - lo].bitcast(FP8X4),
                     rhs_scale=x_scale[:, lo:hi],
                     start=True,
                     stop=True,
@@ -129,29 +141,36 @@ def tile_picked_unet_gelu_e_kernel(tc, xT, w1, w2_words, w2_scales, skip, offs, 
             nc.vector.tensor_copy(up[t][:].indirect(cell_sb[:, cols]), h[:])
 
         z_low = keep.tile([P, 2, U], BF16, name="z_low")
-        z_grouped = keep.tile([P, U, PACK], BF16, name="z_grouped", align_bytes=64)
         first_layer(0, [0, 128])
         first_layer(1, [0, HALF])
         first_layer(0, [128, HALF, S])
         first_layer(1, [HALF, S])
         for t in range(2, PACK):
-            first_layer(t, [0, S])
-        for t in range(2):
-            nc.gpsimd.tensor_tensor(z_low[:, t, :], up[t][:], skip_rows[t], ADD)
-        nc.gpsimd.tensor_tensor(z_high[:, 0, :], up[2][:], skip_rows[2], ADD)
-        for cells in (slice(0, U // 2), slice(U // 2, U)):
+            first_layer(t, [0, HALF, S])
+        nc.gpsimd.tensor_tensor(z_low[:, 0, :], up[0][:], skip_rows[0], ADD)
+        front, back = slice(0, U // 2), slice(U // 2, U)
+        for cells in (front, back):
+            nc.gpsimd.tensor_tensor(z_low[:, 1, cells], up[1][:, cells], skip_rows[1][:, cells], ADD)
             nc.scalar.copy(z_grouped[:, cells, 0:2], z_low[:, :, cells].rearrange("p t v -> p v t"))
+        nc.gpsimd.tensor_tensor(z_third, up[2][:], skip_rows[2], ADD)
 
         z_codes = keep.tile([P, U], U32, name="z_codes", align_bytes=64)
         z_scale = keep.tile([P, U], U8, name="z_scale", align_bytes=64)
         out_blocks = out.rearrange("(b m) v -> m b v", m=P)
         chunks = [slice(c, c + CHUNK) for c in range(0, U, CHUNK)]
 
-        def add_last(cells):
-            nc.vector.tensor_tensor(z_high[:, 1, cells], up[PACK - 1][:, cells], skip_rows[PACK - 1][:, cells], ADD)
+        def staging_run(i):
+            return U // CHUNK + i
 
-        def weave(copy, cells):
-            copy(z_grouped[:, cells, 2:4], z_high[:, 0:2, cells].rearrange("p t v -> p v t"))
+        def add_last(i):
+            cells = slice(chunks[i].start, chunks[i + 1].stop)
+            z_last = halfwords[:, U + cells.start : U + cells.stop]
+            nc.vector.tensor_tensor(z_last, up[PACK - 1][:, cells], skip_rows[PACK - 1][:, cells], ADD)
+
+        def weave(i):
+            copy = nc.scalar.copy if i % 2 == 1 else nc.vector.tensor_copy
+            both = runs[:, i : staging_run(i) + 1 : staging_run(i) - i, :]
+            copy(z_grouped[:, chunks[i], 2:4], both.rearrange("p t v -> p v t"))
 
         def quantize_z(cells):
             nc.vector.quantize_mx(
@@ -173,7 +192,7 @@ def tile_picked_unet_gelu_e_kernel(tc, xT, w1, w2_words, w2_scales, skip, offs, 
 
         def both_blocks(cells):
             quantize_z(cells)
-            acc = psum.tile([P, N // P, CHUNK], F32, name="acc")
+            acc = psum.tile([P, N // P, CHUNK], F32, name="acc", tag="bank")
             for b in range(N // P):
                 second_layer(acc[:, b, :], b, cells)
             return acc
@@ -183,24 +202,34 @@ def tile_picked_unet_gelu_e_kernel(tc, xT, w1, w2_words, w2_scales, skip, offs, 
             copy(result[:], acc[:])
             nc.sync.dma_start(out=out_blocks[:, :, cells], in_=result[:])
 
-        add_last(chunks[0])
-        add_last(chunks[1])
-        weave(nc.vector.tensor_copy, chunks[0])
-        weave(nc.scalar.copy, chunks[1])
-        add_last(chunks[2])
+        def finish(i):
+            leave(nc.scalar.copy, both_blocks(chunks[i]), chunks[i])
+
+        add_last(0)
+        add_last(2)
+        weave(0)
+        weave(1)
+        weave(3)
+        add_last(4)
+        weave(5)
         acc0 = both_blocks(chunks[0])
-        weave(nc.scalar.copy, chunks[2])
-        add_last(chunks[3])
-        acc1 = both_blocks(chunks[1])
+        add_last(6)
+        weave(7)
         leave(nc.scalar.copy, acc0, chunks[0])
-        weave(nc.vector.tensor_copy, chunks[3])
-        acc2 = both_blocks(chunks[2])
-        leave(nc.scalar.copy, acc1, chunks[1])
-        quantize_z(chunks[3])
-        leave(nc.vector.tensor_copy, acc2, chunks[2])
-        last = keep.tile([P, N // P, CHUNK], F32, name="last")
-        for b in range(N // P):
-            acc = psum.tile([P, CHUNK], F32, name="acc")
-            second_layer(acc[:], b, chunks[3])
-            nc.scalar.copy(last[:, b, :], acc[:])
-        nc.sync.dma_start(out=out_blocks[:, :, chunks[3]], in_=last[:])
+        finish(1)
+        weave(2)
+        finish(3)
+        finish(5)
+        weave(4)
+        finish(2)
+        finish(7)
+        weave(6)
+        acc4 = both_blocks(chunks[4])
+        quantize_z(chunks[6])
+        leave(nc.vector.tensor_copy, acc4, chunks[4])
+        result = keep.tile([P, N // P, CHUNK], F32, name="result_last")
+        for b, copy in enumerate((nc.scalar.copy, nc.vector.tensor_copy)):
+            acc = psum.tile([P, CHUNK], F32, name="acc", tag="bank")
+            second_layer(acc[:], b, chunks[6])
+            copy(result[:, b, :], acc[:])
+        nc.sync.dma_start(out=out_blocks[:, :, chunks[6]], in_=result[:])

@@ -1,6 +1,7 @@
 from contextlib import ExitStack
 
 import concourse.mybir as mybir
+from concourse.masks import make_identity
 
 K, T, S, H, N, U = 512, 2048, 512, 512, 256, 1024
 FLOPS = 2 * K * H * S + 2 * H * N * U
@@ -20,35 +21,35 @@ P = 128
 PACK = 4
 LIST_ROWS = 16
 HALF = S // 2
+FIRST = 128
 CHUNK = 128
-AHEAD = 4
 
 
 def tile_picked_unet_gelu_e_kernel(tc, xT, w1, w2_words, w2_scales, skip, offs, cell, out):
     nc = tc.nc
     with ExitStack() as ctx:
         keep = ctx.enter_context(tc.tile_pool(name="keep", bufs=1))
-        psum = ctx.enter_context(tc.psum_pool(name="psum", bufs=8))
+        psum = ctx.enter_context(tc.psum_pool(name="psum", bufs=1))
 
         offs_sb = keep.tile([P, S // LIST_ROWS], U16, name="offs_sb")
         cell_sb = keep.tile([P, S // LIST_ROWS], U16, name="cell_sb")
         w1_raw = [keep.tile([P, PACK, H // 2], F32, name=f"w1_raw{a}", align_bytes=64) for a in range(2)]
         x_rows = [keep.tile([P, T], F32, name=f"x_rows{j}") for j in range(PACK)]
-        work = keep.tile([P, U // 2 + U + 2 * U], F32, name="work", align_bytes=64)
-        skip_rows = [
-            work[:, U // 2 : U // 2 + U] if t == 2 else keep.tile([P, U], F32, name=f"skip_rows{t}")[:] for t in range(PACK)
-        ]
-        halfwords = work[:].bitcast(BF16)
-        z_third = halfwords[:, 0:U]
-        z_grouped = halfwords[:, 3 * U :].rearrange("p (v t) -> p v t", t=PACK)
-        runs = halfwords.rearrange("p (r v) -> p r v", v=CHUNK)
+        z_pairs = keep.tile([P, 2 * U], F32, name="z_pairs", align_bytes=64)
+        z_words = keep.tile([P, 2 * U], F32, name="z_words", align_bytes=64)
+        skip_rows = [keep.tile([P, U], F32, name=f"skip_rows{a}")[:] for a in range(2)] + [z_pairs[:, U:]]
+        z_high = z_pairs[:, U:].bitcast(BF16).rearrange("p (v e) -> p v e", e=2)
         up = [keep.tile([P, U], F32, name=f"up{t}") for t in range(PACK)]
+        up_first = keep.tile([P, U], F32, name="up_first")
         w2_codes = keep.tile([P, 2 * N], U8, name="w2_codes", align_bytes=64)
         w2_scale = keep.tile([P, N], U8, name="w2_scale", align_bytes=64)
 
         nc.vector.memset(w2_scale[:].bitcast(I32), 0)
-        for t in range(PACK):
-            nc.vector.memset(up[t][:], 0.0)
+        for window in (*up, up_first):
+            nc.vector.memset(window[:], 0.0)
+
+        identity = keep.tile([P, P], F32, name="identity")
+        make_identity(nc, identity[:])
 
         warm = keep.tile([P, 1], F32, name="warm")
         nc.scalar.activation(warm[:], up[0][:, 0:1], GELU)
@@ -62,9 +63,15 @@ def tile_picked_unet_gelu_e_kernel(tc, xT, w1, w2_words, w2_scales, skip, offs, 
                 nc.sync.dma_start(offs_sb[:], offs)
         for a in range(2):
             nc.sync.dma_start(out=w1_raw[a][:], in_=w1_planes[:, :, a * H // 2 : (a + 1) * H // 2])
-        nc.sync.dma_start(cell_sb[:], cell)
-        for t in range(PACK):
-            nc.sync.dma_start(out=skip_rows[t], in_=skip_planes[:, t, :])
+            if a == 0:
+                nc.sync.dma_start(cell_sb[:], cell)
+        for a in range(2):
+            for e in range(2):
+                nc.sync.dma_start(
+                    out=skip_rows[a][e * P // 2 : (e + 1) * P // 2, :],
+                    in_=skip_planes[a * P // 2 : (a + 1) * P // 2, e, :],
+                )
+        nc.sync.dma_start(out=skip_rows[2], in_=skip_planes[:, 2, :])
         nc.sync.dma_start(out=w2_codes[:].bitcast(I32), in_=w2_words[0].bitcast(I32))
         for q in range(4):
             nc.sync.dma_start(
@@ -72,7 +79,8 @@ def tile_picked_unet_gelu_e_kernel(tc, xT, w1, w2_words, w2_scales, skip, offs, 
                 in_=w2_scales[0, 4 * q : 4 * q + 4, :].bitcast(I32),
             )
 
-        w1_grouped = keep.tile([P, PACK, P, PACK], BF16, name="w1_grouped", align_bytes=64)
+        w1_first = keep.tile([P, P, PACK], BF16, name="w1_first", align_bytes=64)
+        w1_rest = keep.tile([P, PACK - 1, P, PACK], BF16, name="w1_rest", align_bytes=64)
         w1_codes = keep.tile([P, H], U32, name="w1_codes", align_bytes=64)
         w1_scale = keep.tile([P, H], U8, name="w1_scale", align_bytes=64)
 
@@ -80,103 +88,136 @@ def tile_picked_unet_gelu_e_kernel(tc, xT, w1, w2_words, w2_scales, skip, offs, 
         x_scale = keep.tile([P, S], U8, name="x_scale", align_bytes=64)
         for j in range(PACK - 1):
             nc.vector.tensor_copy(x_grouped[:, :, j], x_rows[j][:].indirect(offs_sb[:]))
-        halves = [slice(0, HALF), slice(HALF, S)]
-        for entries in halves:
-            cols = slice(entries.start // LIST_ROWS, entries.stop // LIST_ROWS)
-            nc.vector.tensor_copy(x_grouped[:, entries, PACK - 1], x_rows[PACK - 1][:].indirect(offs_sb[:, cols]))
+        for first in (0, HALF):
+            cols = slice(first // LIST_ROWS, (first + HALF) // LIST_ROWS)
+            nc.vector.tensor_copy(x_grouped[:, first : first + HALF, PACK - 1], x_rows[PACK - 1][:].indirect(offs_sb[:, cols]))
 
         def quantize_x(codes, entries):
             nc.vector.quantize_mx(
-                out=codes[:].bitcast(FP8X4),
+                out=codes.bitcast(FP8X4),
                 scales=x_scale[:, entries],
                 in_=x_grouped[:, entries, :].rearrange("p s j -> p (s j)"),
             )
 
-        def group_w1(copy, a, tiles):
-            copy(
-                w1_grouped[:, tiles, a * P // 2 : (a + 1) * P // 2, :].rearrange("p t m j -> p m j t"),
-                w1_raw[a][:].rearrange("p j (m t) -> p m j t", t=PACK)[:, :, :, tiles],
+        def w1_columns(a, planes):
+            return w1_raw[a][:].rearrange("p j (m t) -> p m j t", t=PACK)[:, :, :, planes]
+
+        def group_low(copy, a, grouped):
+            copy(grouped.rearrange("p (e m) j -> p m j e", e=2), w1_columns(a, slice(0, 2)))
+
+        def group_high(a):
+            nc.scalar.copy(
+                w1_rest[:, 1:, a * P // 2 : (a + 1) * P // 2, :].rearrange("p t m j -> p m j t"),
+                w1_columns(a, slice(2, PACK)),
             )
 
-        def quantize_w1(tiles):
-            channels = slice(tiles.start * P, tiles.stop * P)
-            nc.vector.quantize_mx(
-                out=w1_codes[:, channels].bitcast(FP8X4),
-                scales=w1_scale[:, channels],
-                in_=w1_grouped[:, tiles, :, :].rearrange("p t m j -> p (t m j)"),
-            )
+        def quantize_w1(first, grouped):
+            channels = slice(first, first + grouped.shape[1] // PACK)
+            nc.vector.quantize_mx(out=w1_codes[:, channels].bitcast(FP8X4), scales=w1_scale[:, channels], in_=grouped)
 
-        x_front = keep.tile([P, HALF], U32, name="x_front", align_bytes=64)
-        quantize_x(x_front, halves[0])
-        low, high = slice(0, 2), slice(2, PACK)
-        group_w1(nc.scalar.copy, 0, low)
-        group_w1(nc.scalar.copy, 0, high)
-        group_w1(nc.vector.tensor_copy, 1, low)
-        group_w1(nc.scalar.copy, 1, high)
-        quantize_w1(slice(0, 1))
-        quantize_w1(slice(1, 2))
-        x_back = keep.tile([P, HALF], U32, name="x_back", tag="w1_raw1", align_bytes=64)
-        quantize_x(x_back, halves[1])
-        quantize_w1(high)
-        x_codes = [x_front, x_back]
+        pieces = [slice(0, FIRST), slice(FIRST, HALF), slice(HALF, S)]
+        x_first = keep.tile([P, FIRST], U32, name="x_first", align_bytes=64)
+        quantize_x(x_first[:], pieces[0])
+        group_low(nc.scalar.copy, 0, w1_first[:])
+        quantize_w1(0, w1_first[:].rearrange("p m j -> p (m j)"))
+        x_rest = keep.tile([P, S - FIRST], U32, name="x_rest", tag="w1_first", align_bytes=64)
+        x_codes = [x_first[:], x_rest[:, 0 : HALF - FIRST], x_rest[:, HALF - FIRST :]]
 
-        def first_layer(t, bounds):
-            first, width = bounds[0], bounds[-1] - bounds[0]
-            entries = slice(bounds[0], bounds[-1])
-            cols = slice(bounds[0] // LIST_ROWS, bounds[-1] // LIST_ROWS)
+        def first_layer(t, group, bank, h):
             channels = slice(t * P, (t + 1) * P)
-            pre = psum.tile([P, width], F32, name="pre", tag="bank")
-            for lo, hi in zip(bounds[:-1], bounds[1:]):
+            first = pieces[group[0]].start
+            pre = psum.tile([P, pieces[group[-1]].stop - first], F32, name="pre", tag=f"bank{bank}")
+            for i in group:
                 nc.tensor.matmul_mx(
-                    out=pre[:, lo - first : hi - first],
+                    out=pre[:, pieces[i].start - first : pieces[i].stop - first],
                     lhsT=w1_codes[:, channels].bitcast(FP8X4),
                     lhsT_scale=w1_scale[:, channels],
-                    rhs=x_codes[lo // HALF][:, lo % HALF : lo % HALF + hi - lo].bitcast(FP8X4),
-                    rhs_scale=x_scale[:, lo:hi],
+                    rhs=x_codes[i].bitcast(FP8X4),
+                    rhs_scale=x_scale[:, pieces[i]],
                     start=True,
                     stop=True,
                 )
-            h = keep.tile([P, width], F32, name=f"h{t}_{entries.start}")
-            nc.scalar.activation(h[:], pre[:], GELU)
-            nc.vector.tensor_copy(up[t][:].indirect(cell_sb[:, cols]), h[:])
+            nc.scalar.activation(h, pre[:], GELU)
 
-        z_low = keep.tile([P, 2, U], BF16, name="z_low")
-        first_layer(0, [0, 128])
-        first_layer(1, [0, HALF])
-        first_layer(0, [128, HALF, S])
-        first_layer(1, [HALF, S])
-        for t in range(2, PACK):
-            first_layer(t, [0, HALF, S])
-        nc.gpsimd.tensor_tensor(z_low[:, 0, :], up[0][:], skip_rows[0], ADD)
-        front, back = slice(0, U // 2), slice(U // 2, U)
-        for cells in (front, back):
-            nc.gpsimd.tensor_tensor(z_low[:, 1, cells], up[1][:, cells], skip_rows[1][:, cells], ADD)
-            nc.scalar.copy(z_grouped[:, cells, 0:2], z_low[:, :, cells].rearrange("p t v -> p v t"))
-        nc.gpsimd.tensor_tensor(z_third, up[2][:], skip_rows[2], ADD)
+        def scatter(window, entries, h):
+            cols = slice(entries.start // LIST_ROWS, entries.stop // LIST_ROWS)
+            nc.vector.tensor_copy(window[:].indirect(cell_sb[:, cols]), h)
+
+        h_front = keep.tile([P, HALF], F32, name="h_front")
+        first_layer(0, [0], 0, h_front[:, pieces[0]])
+        for i in (1, 2):
+            quantize_x(x_codes[i], pieces[i])
+        scatter(up_first, pieces[0], h_front[:, pieces[0]])
+        first_layer(0, [1], 1, h_front[:, pieces[1]])
+        scatter(up[0], pieces[1], h_front[:, pieces[1]])
+        group_low(nc.scalar.copy, 1, w1_rest[:, 0, :, :])
+        quantize_w1(P, w1_rest[:, 0, :, :].rearrange("p m j -> p (m j)"))
+        group_high(0)
+        group_high(1)
+        quantize_w1(2 * P, w1_rest[:, 1:, :, :].rearrange("p t m j -> p (t m j)"))
+        h_back = keep.tile([P, HALF], F32, name="h_back", tag="w1_raw1", align_bytes=64)
+        first_layer(0, [2], 0, h_back[:])
+        scatter(up[0], pieces[2], h_back[:])
+        for t in range(1, PACK):
+            h = keep.tile([P, S], F32, name=f"h{t}")
+            first_layer(t, [0, 1], 2 * t, h[:, 0:HALF])
+            first_layer(t, [2], 2 * t + 1, h[:, HALF:S])
+            scatter(up[t], slice(0, S), h[:])
+
+        blocks = U // 2 // P
+        z_turned = [keep.tile([P, U // 2], F32, name=f"z_turned{c}")[:] for c in range(2)]
+        for a in range(2):
+            for c in range(2):
+                turned = psum.tile([P, blocks, P], F32, name="turned", tag=f"bank{4 + 2 * a + c}")
+                sources = ((skip_rows[0], up_first[:], up[0][:]), (skip_rows[1], up[1][:]))[a]
+                for n, source in enumerate(sources):
+                    for b in range(blocks):
+                        first = (c * blocks + b) * P
+                        nc.tensor.matmul(
+                            turned[:, b, :],
+                            source[:, first : first + P],
+                            identity[:],
+                            start=(n == 0 and b == 0),
+                            stop=(n == len(sources) - 1 and b == blocks - 1),
+                            is_transpose=True,
+                        )
+                pairs = z_turned[c].bitcast(BF16).rearrange("p (b m e) -> p b m e", b=blocks, e=2)
+                nc.scalar.copy(
+                    pairs[:, :, a * P // 2 : (a + 1) * P // 2, :],
+                    turned[:].rearrange("p b (e m) -> p b m e", e=2),
+                )
+        skip_last = keep.tile([P, U], F32, name="skip_last", tag="up1")
+        nc.sync.dma_start(out=skip_last[:], in_=skip_planes[:, PACK - 1, :])
+        for c in range(2):
+            back = psum.tile([P, blocks * P], F32, name="back", tag=f"bank{c}")
+            for b in range(blocks):
+                nc.tensor.transpose(back[:, b * P : (b + 1) * P], z_turned[c][:, b * P : (b + 1) * P], identity[:])
+            nc.scalar.copy(z_pairs[:, c * U // 2 : (c + 1) * U // 2], back[:])
+        for cells in (slice(0, U // 4), slice(U // 4, U)):
+            nc.gpsimd.tensor_tensor(z_high[:, cells, 0], up[2][:, cells], skip_rows[2][:, cells], ADD)
+        nc.scalar.copy(
+            z_words[:].rearrange("p (v u) -> p v u", u=2)[:, 0:CHUNK, :],
+            z_pairs[:].rearrange("p (u v) -> p v u", u=2)[:, 0:CHUNK, :],
+        )
 
         z_codes = keep.tile([P, U], U32, name="z_codes", align_bytes=64)
         z_scale = keep.tile([P, U], U8, name="z_scale", align_bytes=64)
         out_blocks = out.rearrange("(b m) v -> m b v", m=P)
-        chunks = [slice(c, c + CHUNK) for c in range(0, U, CHUNK)]
 
-        def staging_run(i):
-            return U // CHUNK + i
+        def add_last(cells):
+            nc.vector.tensor_tensor(z_high[:, cells, 1], up[PACK - 1][:, cells], skip_last[:, cells], ADD)
 
-        def add_last(i):
-            cells = slice(chunks[i].start, chunks[i + 1].stop)
-            z_last = halfwords[:, U + cells.start : U + cells.stop]
-            nc.vector.tensor_tensor(z_last, up[PACK - 1][:, cells], skip_rows[PACK - 1][:, cells], ADD)
-
-        def weave(i):
-            copy = nc.scalar.copy if i % 2 == 1 else nc.vector.tensor_copy
-            both = runs[:, i : staging_run(i) + 1 : staging_run(i) - i, :]
-            copy(z_grouped[:, chunks[i], 2:4], both.rearrange("p t v -> p v t"))
+        def weave(copy, cells):
+            copy(
+                z_words[:].rearrange("p (v u) -> p v u", u=2)[:, cells, :],
+                z_pairs[:].rearrange("p (u v) -> p v u", u=2)[:, cells, :],
+            )
 
         def quantize_z(cells):
             nc.vector.quantize_mx(
                 out=z_codes[:, cells].bitcast(FP8X4),
                 scales=z_scale[:, cells],
-                in_=z_grouped[:, cells, :].rearrange("p v t -> p (v t)"),
+                in_=z_words[:, 2 * cells.start : 2 * cells.stop].bitcast(BF16),
             )
 
         def second_layer(acc, b, cells):
@@ -190,46 +231,44 @@ def tile_picked_unet_gelu_e_kernel(tc, xT, w1, w2_words, w2_scales, skip, offs, 
                 stop=True,
             )
 
-        def both_blocks(cells):
-            quantize_z(cells)
-            acc = psum.tile([P, N // P, CHUNK], F32, name="acc", tag="bank")
+        def leave(copy, cells, bank):
+            width = cells.stop - cells.start
+            acc = psum.tile([P, N // P, width], F32, name="acc", tag=f"bank{bank}")
             for b in range(N // P):
                 second_layer(acc[:, b, :], b, cells)
-            return acc
-
-        def leave(copy, acc, cells):
-            result = keep.tile([P, N // P, CHUNK], F32, name=f"result{cells.start}")
+            result = keep.tile([P, N // P, width], F32, name=f"result{cells.start}")
             copy(result[:], acc[:])
             nc.sync.dma_start(out=out_blocks[:, :, cells], in_=result[:])
 
-        def finish(i):
-            leave(nc.scalar.copy, both_blocks(chunks[i]), chunks[i])
+        def leave_by_blocks(cells, banks):
+            width = cells.stop - cells.start
+            result = keep.tile([P, N // P, width], F32, name=f"result{cells.start}")
+            for b, copy in enumerate((nc.scalar.copy, nc.vector.tensor_copy)):
+                acc = psum.tile([P, width], F32, name="acc", tag=f"bank{banks[b]}")
+                second_layer(acc[:], b, cells)
+                copy(result[:, b, :], acc[:])
+            nc.sync.dma_start(out=out_blocks[:, :, cells], in_=result[:])
 
-        add_last(0)
-        add_last(2)
-        weave(0)
-        weave(1)
-        weave(3)
-        add_last(4)
-        weave(5)
-        acc0 = both_blocks(chunks[0])
-        add_last(6)
-        weave(7)
-        leave(nc.scalar.copy, acc0, chunks[0])
-        finish(1)
-        weave(2)
-        finish(3)
-        finish(5)
-        weave(4)
-        finish(2)
-        finish(7)
-        weave(6)
-        acc4 = both_blocks(chunks[4])
-        quantize_z(chunks[6])
-        leave(nc.vector.tensor_copy, acc4, chunks[4])
-        result = keep.tile([P, N // P, CHUNK], F32, name="result_last")
-        for b, copy in enumerate((nc.scalar.copy, nc.vector.tensor_copy)):
-            acc = psum.tile([P, CHUNK], F32, name="acc", tag="bank")
-            second_layer(acc[:], b, chunks[6])
-            copy(result[:, b, :], acc[:])
-        nc.sync.dma_start(out=out_blocks[:, :, chunks[6]], in_=result[:])
+        on_scalar, on_vector = nc.scalar.copy, nc.vector.tensor_copy
+        c = [slice(i, i + CHUNK) for i in range(0, U, CHUNK)]
+        nc.vector.tensor_tensor(
+            z_words[:].bitcast(BF16).rearrange("p (v t) -> p v t", t=PACK)[:, c[0], PACK - 1],
+            up[PACK - 1][:, c[0]],
+            skip_last[:, c[0]],
+            ADD,
+        )
+        add_last(c[1])
+        weave(on_scalar, c[1])
+        quantize_z(c[0])
+        leave(on_scalar, c[0], 0)
+        for i in range(2, len(c), 2):
+            add_last(c[i])
+            add_last(c[i + 1])
+            weave(on_vector, c[i])
+            weave(on_scalar, c[i + 1])
+            quantize_z(c[i - 1])
+            leave(on_scalar, c[i - 1], i - 1)
+            quantize_z(c[i])
+            leave(on_scalar, c[i], i)
+        quantize_z(c[7])
+        leave_by_blocks(c[7], (7, 0))

@@ -240,17 +240,20 @@ def tile_picked_unet_gelu_e_kernel(tc, xT, w1, w2_words, w2_scales, skip, offs, 
             copy(result[:], acc[:])
             nc.sync.dma_start(out=out_blocks[:, :, cells], in_=result[:])
 
-        def leave_by_blocks(cells, banks):
+        def leave_block(copy, cells, b, bank):
             width = cells.stop - cells.start
-            result = keep.tile([P, N // P, width], F32, name=f"result{cells.start}")
-            for b, copy in enumerate((nc.scalar.copy, nc.vector.tensor_copy)):
-                acc = psum.tile([P, width], F32, name="acc", tag=f"bank{banks[b]}")
-                second_layer(acc[:], b, cells)
-                copy(result[:, b, :], acc[:])
-            nc.sync.dma_start(out=out_blocks[:, :, cells], in_=result[:])
+            acc = psum.tile([P, width], F32, name="acc", tag=f"bank{bank}")
+            second_layer(acc[:], b, cells)
+            result = keep.tile([P, width], F32, name=f"result{cells.start}_{b}")
+            copy(result[:], acc[:])
+            nc.sync.dma_start(out=out_blocks[:, b, cells], in_=result[:])
 
         on_scalar, on_vector = nc.scalar.copy, nc.vector.tensor_copy
         c = [slice(i, i + CHUNK) for i in range(0, U, CHUNK)]
+
+        def pair(i):
+            return slice(c[i].start, c[i + 1].stop)
+
         nc.vector.tensor_tensor(
             z_words[:].bitcast(BF16).rearrange("p (v t) -> p v t", t=PACK)[:, c[0], PACK - 1],
             up[PACK - 1][:, c[0]],
@@ -260,15 +263,26 @@ def tile_picked_unet_gelu_e_kernel(tc, xT, w1, w2_words, w2_scales, skip, offs, 
         add_last(c[1])
         weave(on_scalar, c[1])
         quantize_z(c[0])
-        leave(on_scalar, c[0], 0)
-        for i in range(2, len(c), 2):
-            add_last(c[i])
-            add_last(c[i + 1])
-            weave(on_vector, c[i])
-            weave(on_scalar, c[i + 1])
-            quantize_z(c[i - 1])
-            leave(on_scalar, c[i - 1], i - 1)
-            quantize_z(c[i])
-            leave(on_scalar, c[i], i)
+        for b in range(N // P):
+            leave_block(on_scalar, c[0], b, 6 + b)
+        add_last(pair(2))
+        weave(on_scalar, c[3])
+        quantize_z(c[1])
+        leave(on_scalar, c[1], 1)
+        weave(on_vector, c[2])
+        add_last(pair(4))
+        weave(on_scalar, c[5])
+        quantize_z(pair(2))
+        for b in range(N // P):
+            leave_block(on_scalar, pair(2), b, 2 + b)
+        weave(on_vector, c[4])
+        add_last(pair(6))
+        quantize_z(pair(4))
+        for b in range(N // P):
+            leave_block(on_scalar, pair(4), b, 4 + b)
+        weave(on_vector, pair(6))
+        quantize_z(c[6])
         quantize_z(c[7])
-        leave_by_blocks(c[7], (7, 0))
+        leave(on_vector, c[6], 6)
+        leave_block(on_scalar, c[7], 0, 7)
+        leave_block(on_vector, c[7], 1, 0)

@@ -61,10 +61,11 @@ def tile_picked_unet_gelu_e_kernel(tc, xT, w1, w2_words, w2_scales, skip, offs, 
             nc.sync.dma_start(out=x_rows[j][:], in_=x_planes[:, j, :])
             if j == 0:
                 nc.sync.dma_start(offs_sb[:], offs)
-        for a in range(2):
-            nc.sync.dma_start(out=w1_raw[a][:], in_=w1_planes[:, :, a * H // 2 : (a + 1) * H // 2])
-            if a == 0:
-                nc.sync.dma_start(cell_sb[:], cell)
+        row_pairs = (slice(0, 2), slice(2, PACK))
+        for rows in row_pairs:
+            nc.sync.dma_start(out=w1_raw[0][:, rows, :], in_=w1_planes[:, rows, 0 : H // 2])
+        nc.sync.dma_start(cell_sb[:], cell)
+        nc.sync.dma_start(out=w1_raw[1][:], in_=w1_planes[:, :, H // 2 : H])
         for a in range(2):
             for e in range(2):
                 nc.sync.dma_start(
@@ -102,14 +103,19 @@ def tile_picked_unet_gelu_e_kernel(tc, xT, w1, w2_words, w2_scales, skip, offs, 
         def w1_columns(a, planes):
             return w1_raw[a][:].rearrange("p j (m t) -> p m j t", t=PACK)[:, :, :, planes]
 
-        def group_low(copy, a, grouped):
-            copy(grouped.rearrange("p (e m) j -> p m j e", e=2), w1_columns(a, slice(0, 2)))
+        def group_low(a, grouped, rows):
+            nc.scalar.copy(
+                grouped.rearrange("p (e m) j -> p m j e", e=2)[:, :, rows, :], w1_columns(a, slice(0, 2))[:, :, rows, :]
+            )
 
         def group_high(a):
             nc.scalar.copy(
                 w1_rest[:, 1:, a * P // 2 : (a + 1) * P // 2, :].rearrange("p t m j -> p m j t"),
                 w1_columns(a, slice(2, PACK)),
             )
+            for t in range(2, PACK):
+                quads = slice(a * P // 2, (a + 1) * P // 2)
+                quantize_w1(t * P + quads.start, w1_rest[:, t - 1, quads, :].rearrange("p m j -> p (m j)"))
 
         def quantize_w1(first, grouped):
             channels = slice(first, first + grouped.shape[1] // PACK)
@@ -118,7 +124,8 @@ def tile_picked_unet_gelu_e_kernel(tc, xT, w1, w2_words, w2_scales, skip, offs, 
         pieces = [slice(0, FIRST), slice(FIRST, HALF), slice(HALF, S)]
         x_first = keep.tile([P, FIRST], U32, name="x_first", align_bytes=64)
         quantize_x(x_first[:], pieces[0])
-        group_low(nc.scalar.copy, 0, w1_first[:])
+        for rows in row_pairs:
+            group_low(0, w1_first[:], rows)
         quantize_w1(0, w1_first[:].rearrange("p m j -> p (m j)"))
         x_rest = keep.tile([P, S - FIRST], U32, name="x_rest", tag="w1_first", align_bytes=64)
         x_codes = [x_first[:], x_rest[:, 0 : HALF - FIRST], x_rest[:, HALF - FIRST :]]
@@ -147,14 +154,13 @@ def tile_picked_unet_gelu_e_kernel(tc, xT, w1, w2_words, w2_scales, skip, offs, 
         first_layer(0, [0], 0, h_front[:, pieces[0]])
         for i in (1, 2):
             quantize_x(x_codes[i], pieces[i])
+        group_high(0)
         scatter(up_first, pieces[0], h_front[:, pieces[0]])
         first_layer(0, [1], 1, h_front[:, pieces[1]])
         scatter(up[0], pieces[1], h_front[:, pieces[1]])
-        group_low(nc.scalar.copy, 1, w1_rest[:, 0, :, :])
+        group_low(1, w1_rest[:, 0, :, :], slice(0, PACK))
         quantize_w1(P, w1_rest[:, 0, :, :].rearrange("p m j -> p (m j)"))
-        group_high(0)
         group_high(1)
-        quantize_w1(2 * P, w1_rest[:, 1:, :, :].rearrange("p t m j -> p (t m j)"))
         h_back = keep.tile([P, HALF], F32, name="h_back", tag="w1_raw1", align_bytes=64)
         first_layer(0, [2], 0, h_back[:])
         scatter(up[0], pieces[2], h_back[:])

@@ -73,6 +73,8 @@ def tile_picked_unet_gelu_e_kernel(tc, xT, w1, w2_words, w2_scales, skip, offs, 
                     in_=skip_planes[a * P // 2 : (a + 1) * P // 2, e, :],
                 )
         nc.sync.dma_start(out=skip_rows[2], in_=skip_planes[:, 2, :])
+        skip_last = keep.tile([P, 3 * U // 4], F32, name="skip_last")
+        nc.sync.dma_start(out=skip_last[:], in_=skip_planes[:, PACK - 1, 0 : 3 * U // 4])
         nc.sync.dma_start(out=w2_codes[:].bitcast(I32), in_=w2_words[0].bitcast(I32))
         for q in range(4):
             nc.sync.dma_start(
@@ -171,6 +173,15 @@ def tile_picked_unet_gelu_e_kernel(tc, xT, w1, w2_words, w2_scales, skip, offs, 
             scatter(up[t], slice(0, S), h[:])
 
         blocks = U // 2 // P
+        banked = (0, 1, 4, 5)
+        skip_there = psum.tile([P, blocks, P], F32, name="skip_there", tag="bank2")
+        for n, i in enumerate(banked):
+            nc.tensor.transpose(skip_there[:, n, :], skip_last[:, i * P : (i + 1) * P], identity[:])
+        skip_turned = keep.tile([P, blocks, P], F32, name="skip_turned")
+        nc.scalar.copy(skip_turned[:], skip_there[:])
+        skip_bank = psum.tile([P, blocks * P], F32, name="skip_bank", tag="bank3")
+        for n in range(blocks):
+            nc.tensor.transpose(skip_bank[:, n * P : (n + 1) * P], skip_turned[:, n, :], identity[:])
         z_turned = [keep.tile([P, U // 2], F32, name=f"z_turned{c}")[:] for c in range(2)]
         for a in range(2):
             for c in range(2):
@@ -192,26 +203,33 @@ def tile_picked_unet_gelu_e_kernel(tc, xT, w1, w2_words, w2_scales, skip, offs, 
                     pairs[:, :, a * P // 2 : (a + 1) * P // 2, :],
                     turned[:].rearrange("p b (e m) -> p b m e", e=2),
                 )
-        skip_last = keep.tile([P, U], F32, name="skip_last", tag="up1")
-        nc.sync.dma_start(out=skip_last[:], in_=skip_planes[:, PACK - 1, :])
         for c in range(2):
             back = psum.tile([P, blocks * P], F32, name="back", tag=f"bank{c}")
             for b in range(blocks):
                 nc.tensor.transpose(back[:, b * P : (b + 1) * P], z_turned[c][:, b * P : (b + 1) * P], identity[:])
             nc.scalar.copy(z_pairs[:, c * U // 2 : (c + 1) * U // 2], back[:])
-        for cells in (slice(0, U // 4), slice(U // 4, U)):
+        woven = z_words[:].rearrange("p (v u) -> p v u", u=2)
+        paired = z_pairs[:].rearrange("p (u v) -> p v u", u=2)
+        c = [slice(i, i + CHUNK) for i in range(0, U, CHUNK)]
+
+        def pair(i):
+            return slice(c[i].start, c[i + 1].stop)
+
+        skip_end = keep.tile([P, U // 4], F32, name="skip_end", tag="z_turned1")
+        nc.sync.dma_start(out=skip_end[:], in_=skip_planes[:, PACK - 1, pair(6)])
+        for cells in (slice(0, U // 2), slice(U // 2, U)):
             nc.gpsimd.tensor_tensor(z_high[:, cells, 0], up[2][:, cells], skip_rows[2][:, cells], ADD)
-        nc.scalar.copy(
-            z_words[:].rearrange("p (v u) -> p v u", u=2)[:, 0:CHUNK, :],
-            z_pairs[:].rearrange("p (u v) -> p v u", u=2)[:, 0:CHUNK, :],
-        )
+        for cells in (pair(2), c[0], c[1]):
+            nc.scalar.copy(woven[:, cells, :], paired[:, cells, :])
 
         z_codes = keep.tile([P, U], U32, name="z_codes", align_bytes=64)
         z_scale = keep.tile([P, U], U8, name="z_scale", align_bytes=64)
         out_blocks = out.rearrange("(b m) v -> m b v", m=P)
 
-        def add_last(cells):
-            nc.vector.tensor_tensor(z_high[:, cells, 1], up[PACK - 1][:, cells], skip_last[:, cells], ADD)
+        z_last = z_words[:].bitcast(BF16).rearrange("p (v t) -> p v t", t=PACK)[:, :, PACK - 1]
+
+        def add_last(engine, target, cells, addend):
+            engine.tensor_tensor(target[:, cells], up[PACK - 1][:, cells], addend, ADD)
 
         def weave(copy, cells):
             copy(
@@ -255,40 +273,26 @@ def tile_picked_unet_gelu_e_kernel(tc, xT, w1, w2_words, w2_scales, skip, offs, 
             nc.sync.dma_start(out=out_blocks[:, b, cells], in_=result[:])
 
         on_scalar, on_vector = nc.scalar.copy, nc.vector.tensor_copy
-        c = [slice(i, i + CHUNK) for i in range(0, U, CHUNK)]
+        staged = z_high[:, :, 1]
 
-        def pair(i):
-            return slice(c[i].start, c[i + 1].stop)
-
-        nc.vector.tensor_tensor(
-            z_words[:].bitcast(BF16).rearrange("p (v t) -> p v t", t=PACK)[:, c[0], PACK - 1],
-            up[PACK - 1][:, c[0]],
-            skip_last[:, c[0]],
-            ADD,
-        )
-        add_last(c[1])
-        weave(on_scalar, c[1])
+        add_last(nc.gpsimd, z_last, pair(2), skip_last[:, pair(2)])
+        add_last(nc.vector, z_last, c[0], skip_bank[:, c[0]])
+        add_last(nc.vector, staged, pair(4), skip_bank[:, pair(2)])
+        add_last(nc.vector, z_last, c[1], skip_bank[:, c[1]])
+        weave(on_scalar, pair(4))
         quantize_z(c[0])
         for b in range(N // P):
             leave_block(on_scalar, c[0], b, 6 + b)
-        add_last(pair(2))
-        weave(on_scalar, c[3])
-        quantize_z(c[1])
-        leave(on_scalar, c[1], 1)
-        weave(on_vector, c[2])
-        add_last(pair(4))
-        weave(on_scalar, c[5])
         quantize_z(pair(2))
         for b in range(N // P):
-            leave_block(on_scalar, pair(2), b, 2 + b)
-        weave(on_vector, c[4])
-        add_last(pair(6))
+            leave_block(on_scalar, pair(2), b, b)
+        add_last(nc.vector, staged, pair(6), skip_end[:])
         quantize_z(pair(4))
-        for b in range(N // P):
-            leave_block(on_scalar, pair(4), b, 4 + b)
         weave(on_vector, pair(6))
-        quantize_z(c[6])
-        quantize_z(c[7])
-        leave(on_vector, c[6], 6)
-        leave_block(on_scalar, c[7], 0, 7)
-        leave_block(on_vector, c[7], 1, 0)
+        quantize_z(c[1])
+        quantize_z(pair(6))
+        leave_block(on_scalar, pair(4), 0, 4)
+        leave_block(on_vector, pair(4), 1, 5)
+        leave(on_scalar, c[1], 2)
+        leave_block(on_scalar, pair(6), 0, 6)
+        leave_block(on_vector, pair(6), 1, 7)

@@ -219,7 +219,7 @@ def tile_picked_unet_gelu_e_kernel(tc, xT, w1, w2_words, w2_scales, skip, offs, 
         nc.sync.dma_start(out=skip_end[:], in_=skip_planes[:, PACK - 1, pair(6)])
         for cells in (slice(0, U // 2), slice(U // 2, U)):
             nc.gpsimd.tensor_tensor(z_high[:, cells, 0], up[2][:, cells], skip_rows[2][:, cells], ADD)
-        for cells in (pair(2), c[0], c[1]):
+        for cells in (pair(2), c[0]):
             nc.scalar.copy(woven[:, cells, :], paired[:, cells, :])
 
         z_codes = keep.tile([P, U], U32, name="z_codes", align_bytes=64)
@@ -278,7 +278,7 @@ def tile_picked_unet_gelu_e_kernel(tc, xT, w1, w2_words, w2_scales, skip, offs, 
         add_last(nc.gpsimd, z_last, pair(2), skip_last[:, pair(2)])
         add_last(nc.vector, z_last, c[0], skip_bank[:, c[0]])
         add_last(nc.vector, staged, pair(4), skip_bank[:, pair(2)])
-        add_last(nc.vector, z_last, c[1], skip_bank[:, c[1]])
+        add_last(nc.vector, staged, c[1], skip_bank[:, c[1]])
         weave(on_scalar, pair(4))
         quantize_z(c[0])
         for b in range(N // P):
@@ -287,6 +287,7 @@ def tile_picked_unet_gelu_e_kernel(tc, xT, w1, w2_words, w2_scales, skip, offs, 
         for b in range(N // P):
             leave_block(on_scalar, pair(2), b, b)
         add_last(nc.vector, staged, pair(6), skip_end[:])
+        weave(on_vector, c[1])
         quantize_z(pair(4))
         weave(on_vector, pair(6))
         quantize_z(c[1])

@@ -16,13 +16,16 @@ FP8X4 = mybir.dt.float8_e4m3fn_x4
 FP4X4 = mybir.dt.float4_e2m1fn_x4
 ADD = mybir.AluOpType.add
 GELU = mybir.ActivationFunctionType.Gelu_apprx_tanh
+COPY = mybir.ActivationFunctionType.Copy
 
 P = 128
 PACK = 4
 LIST_ROWS = 16
 HALF = S // 2
 FIRST = 128
-CHUNK = 128
+SIDE = U // 2
+SHARE = 192
+CHUNK = 256
 
 
 def tile_picked_unet_gelu_e_kernel(tc, xT, w1, w2_words, w2_scales, skip, offs, cell, out):
@@ -33,19 +36,17 @@ def tile_picked_unet_gelu_e_kernel(tc, xT, w1, w2_words, w2_scales, skip, offs, 
 
         offs_sb = keep.tile([P, S // LIST_ROWS], U16, name="offs_sb")
         cell_sb = keep.tile([P, S // LIST_ROWS], U16, name="cell_sb")
-        w1_raw = [keep.tile([P, PACK, H // 2], F32, name=f"w1_raw{a}", align_bytes=64) for a in range(2)]
         x_rows = [keep.tile([P, T], F32, name=f"x_rows{j}") for j in range(PACK)]
-        z_pairs = keep.tile([P, 2 * U], F32, name="z_pairs", align_bytes=64)
-        z_words = keep.tile([P, 2 * U], F32, name="z_words", align_bytes=64)
-        skip_rows = [keep.tile([P, U], F32, name=f"skip_rows{a}")[:] for a in range(2)] + [z_pairs[:, U:]]
-        z_high = z_pairs[:, U:].bitcast(BF16).rearrange("p (v e) -> p v e", e=2)
-        up = [keep.tile([P, U], F32, name=f"up{t}") for t in range(PACK)]
-        up_first = keep.tile([P, U], F32, name="up_first")
+        w1_raw = [keep.tile([P, PACK, H // 2], F32, name=f"w1_raw{a}") for a in range(2)]
+        z_pairs = keep.tile([P, 2 * U], F32, name="z_pairs")
+        skip_low = [keep.tile([P, U], F32, name=f"skip_low{a}") for a in range(2)]
+        skip_high = [keep.tile([P, U], F32, name=f"skip_high{e}") for e in range(2)]
+        up = [keep.tile([P, U], F32, name=f"up{t}") for t in range(PACK + 1)]
         w2_codes = keep.tile([P, 2 * N], U8, name="w2_codes", align_bytes=64)
         w2_scale = keep.tile([P, N], U8, name="w2_scale", align_bytes=64)
 
         nc.vector.memset(w2_scale[:].bitcast(I32), 0)
-        for window in (*up, up_first):
+        for window in up:
             nc.vector.memset(window[:], 0.0)
 
         identity = keep.tile([P, P], F32, name="identity")
@@ -69,12 +70,11 @@ def tile_picked_unet_gelu_e_kernel(tc, xT, w1, w2_words, w2_scales, skip, offs, 
         for a in range(2):
             for e in range(2):
                 nc.sync.dma_start(
-                    out=skip_rows[a][e * P // 2 : (e + 1) * P // 2, :],
+                    out=skip_low[a][e * P // 2 : (e + 1) * P // 2, :],
                     in_=skip_planes[a * P // 2 : (a + 1) * P // 2, e, :],
                 )
-        nc.sync.dma_start(out=skip_rows[2], in_=skip_planes[:, 2, :])
-        skip_last = keep.tile([P, 3 * U // 4], F32, name="skip_last")
-        nc.sync.dma_start(out=skip_last[:], in_=skip_planes[:, PACK - 1, 0 : 3 * U // 4])
+        for e in (1, 0):
+            nc.sync.dma_start(out=skip_high[e][:], in_=skip_planes[:, 2 + e, :])
         nc.sync.dma_start(out=w2_codes[:].bitcast(I32), in_=w2_words[0].bitcast(I32))
         for q in range(4):
             nc.sync.dma_start(
@@ -82,12 +82,8 @@ def tile_picked_unet_gelu_e_kernel(tc, xT, w1, w2_words, w2_scales, skip, offs, 
                 in_=w2_scales[0, 4 * q : 4 * q + 4, :].bitcast(I32),
             )
 
-        w1_first = keep.tile([P, P, PACK], BF16, name="w1_first", align_bytes=64)
-        w1_rest = keep.tile([P, PACK - 1, P, PACK], BF16, name="w1_rest", align_bytes=64)
-        w1_codes = keep.tile([P, H], U32, name="w1_codes", align_bytes=64)
-        w1_scale = keep.tile([P, H], U8, name="w1_scale", align_bytes=64)
-
         x_grouped = keep.tile([P, S, PACK], BF16, name="x_grouped", align_bytes=64)
+        x_codes = keep.tile([P, S], U32, name="x_codes", align_bytes=64)
         x_scale = keep.tile([P, S], U8, name="x_scale", align_bytes=64)
         for j in range(PACK - 1):
             nc.vector.tensor_copy(x_grouped[:, :, j], x_rows[j][:].indirect(offs_sb[:]))
@@ -95,147 +91,187 @@ def tile_picked_unet_gelu_e_kernel(tc, xT, w1, w2_words, w2_scales, skip, offs, 
             cols = slice(first // LIST_ROWS, (first + HALF) // LIST_ROWS)
             nc.vector.tensor_copy(x_grouped[:, first : first + HALF, PACK - 1], x_rows[PACK - 1][:].indirect(offs_sb[:, cols]))
 
-        def quantize_x(codes, entries):
+        def quantize_x(first, last):
             nc.vector.quantize_mx(
-                out=codes.bitcast(FP8X4),
-                scales=x_scale[:, entries],
-                in_=x_grouped[:, entries, :].rearrange("p s j -> p (s j)"),
+                out=x_codes[:, first:last].bitcast(FP8X4),
+                scales=x_scale[:, first:last],
+                in_=x_grouped[:, first:last, :].rearrange("p s j -> p (s j)"),
             )
 
-        def w1_columns(a, planes):
-            return w1_raw[a][:].rearrange("p j (m t) -> p m j t", t=PACK)[:, :, :, planes]
+        w1_low = [keep.tile([P, P, PACK], BF16, name=f"w1_low{a}", align_bytes=64) for a in range(2)]
+        w1_high = keep.tile([P, 2, P, PACK], BF16, name="w1_high", align_bytes=64)
+        w1_grouped = [w1_low[0][:], w1_low[1][:], w1_high[:, 0, :, :], w1_high[:, 1, :, :]]
+        w1_codes = [keep.tile([P, P], U32, name=f"w1_codes{t}", align_bytes=64) for t in range(PACK)]
+        w1_scale = [keep.tile([P, P], U8, name=f"w1_scale{t}", align_bytes=64) for t in range(PACK)]
 
-        def group_low(a, grouped, rows):
-            nc.scalar.copy(
-                grouped.rearrange("p (e m) j -> p m j e", e=2)[:, :, rows, :], w1_columns(a, slice(0, 2))[:, :, rows, :]
+        def group_low(copy, a, rows, order):
+            copy(
+                w1_low[a][:].rearrange("p (e m) j -> p e m j", e=2)[:, :, :, rows].rearrange(f"p e m j -> {order}"),
+                w1_raw[a][:].rearrange("p j (m t) -> p t m j", t=PACK)[:, 0:2, :, rows].rearrange(f"p e m j -> {order}"),
             )
 
         def group_high(a):
             nc.scalar.copy(
-                w1_rest[:, 1:, a * P // 2 : (a + 1) * P // 2, :].rearrange("p t m j -> p m j t"),
-                w1_columns(a, slice(2, PACK)),
+                w1_high[:, :, a * P // 2 : (a + 1) * P // 2, :].rearrange("p t m j -> p m j t"),
+                w1_raw[a][:].rearrange("p j (m t) -> p m j t", t=PACK)[:, :, :, 2:PACK],
             )
-            for t in range(2, PACK):
-                quads = slice(a * P // 2, (a + 1) * P // 2)
-                quantize_w1(t * P + quads.start, w1_rest[:, t - 1, quads, :].rearrange("p m j -> p (m j)"))
 
-        def quantize_w1(first, grouped):
-            channels = slice(first, first + grouped.shape[1] // PACK)
-            nc.vector.quantize_mx(out=w1_codes[:, channels].bitcast(FP8X4), scales=w1_scale[:, channels], in_=grouped)
+        def quantize_w1(t):
+            nc.vector.quantize_mx(
+                out=w1_codes[t][:].bitcast(FP8X4),
+                scales=w1_scale[t][:],
+                in_=w1_grouped[t].rearrange("p m j -> p (m j)"),
+            )
 
-        pieces = [slice(0, FIRST), slice(FIRST, HALF), slice(HALF, S)]
-        x_first = keep.tile([P, FIRST], U32, name="x_first", align_bytes=64)
-        quantize_x(x_first[:], pieces[0])
+        on_scalar, on_vector = nc.scalar.copy, nc.vector.tensor_copy
+        h = [keep.tile([P, S], F32, name=f"h{t}", align_bytes=64) for t in range(PACK)]
+        h_late = []
+        h_share = keep.tile([P, SHARE], F32, name="h_share")
+
+        def values(t, first, last):
+            if t == 0 and first >= FIRST:
+                return h_late[0][:, first:last]
+            if t == 1 and last <= SHARE:
+                return h_share[:, first:last]
+            return h[t][:, first:last]
+
+        def first_layer(bank, *parts):
+            pre = psum.tile([P, S], F32, name="pre", tag=f"bank{bank}")
+            places = []
+            for t, cuts in parts:
+                place = places[-1].stop if places else 0
+                places.append(slice(place, place + cuts[-1] - cuts[0]))
+                for first, last in zip(cuts, cuts[1:]):
+                    nc.tensor.matmul_mx(
+                        out=pre[:, place + first - cuts[0] : place + last - cuts[0]],
+                        lhsT=w1_codes[t][:].bitcast(FP8X4),
+                        lhsT_scale=w1_scale[t][:],
+                        rhs=x_codes[:, first:last].bitcast(FP8X4),
+                        rhs_scale=x_scale[:, first:last],
+                        start=True,
+                        stop=True,
+                    )
+            for (t, cuts), place in zip(parts, places):
+                nc.scalar.activation(values(t, cuts[0], cuts[-1]), pre[:, place], GELU)
+
+        def window(t, first, last):
+            return up[t][:].indirect(cell_sb[:, first // LIST_ROWS : last // LIST_ROWS])
+
+        def scatter_on_vector(t, first, last):
+            nc.vector.tensor_copy(window(t, first, last), values(t, first, last))
+
+        def scatter_on_scalar(t, first, last, w):
+            nc.scalar.activation(window(w, first, last), values(t, first, last), COPY)
+
+        quantize_x(0, FIRST)
         for rows in row_pairs:
-            group_low(0, w1_first[:], rows)
-        quantize_w1(0, w1_first[:].rearrange("p m j -> p (m j)"))
-        x_rest = keep.tile([P, S - FIRST], U32, name="x_rest", tag="w1_first", align_bytes=64)
-        x_codes = [x_first[:], x_rest[:, 0 : HALF - FIRST], x_rest[:, HALF - FIRST :]]
-
-        def first_layer(t, group, bank, h):
-            channels = slice(t * P, (t + 1) * P)
-            first = pieces[group[0]].start
-            pre = psum.tile([P, pieces[group[-1]].stop - first], F32, name="pre", tag=f"bank{bank}")
-            for i in group:
-                nc.tensor.matmul_mx(
-                    out=pre[:, pieces[i].start - first : pieces[i].stop - first],
-                    lhsT=w1_codes[:, channels].bitcast(FP8X4),
-                    lhsT_scale=w1_scale[:, channels],
-                    rhs=x_codes[i].bitcast(FP8X4),
-                    rhs_scale=x_scale[:, pieces[i]],
-                    start=True,
-                    stop=True,
-                )
-            nc.scalar.activation(h, pre[:], GELU)
-
-        def scatter(window, entries, h):
-            cols = slice(entries.start // LIST_ROWS, entries.stop // LIST_ROWS)
-            nc.vector.tensor_copy(window[:].indirect(cell_sb[:, cols]), h)
-
-        h_front = keep.tile([P, HALF], F32, name="h_front")
-        first_layer(0, [0], 0, h_front[:, pieces[0]])
-        for i in (1, 2):
-            quantize_x(x_codes[i], pieces[i])
+            group_low(on_scalar, 0, rows, "p m j e")
+        quantize_w1(0)
+        quantize_x(FIRST, HALF)
+        quantize_x(HALF, S)
         group_high(0)
-        scatter(up_first, pieces[0], h_front[:, pieces[0]])
-        first_layer(0, [1], 1, h_front[:, pieces[1]])
-        scatter(up[0], pieces[1], h_front[:, pieces[1]])
-        group_low(1, w1_rest[:, 0, :, :], slice(0, PACK))
-        quantize_w1(P, w1_rest[:, 0, :, :].rearrange("p m j -> p (m j)"))
+        first_layer(0, (0, (0, FIRST)))
+        scatter_on_vector(0, 0, FIRST)
+        group_low(nc.gpsimd.tensor_copy, 1, slice(0, PACK), "p e m j")
         group_high(1)
-        h_back = keep.tile([P, HALF], F32, name="h_back", tag="w1_raw1", align_bytes=64)
-        first_layer(0, [2], 0, h_back[:])
-        scatter(up[0], pieces[2], h_back[:])
-        for t in range(1, PACK):
-            h = keep.tile([P, S], F32, name=f"h{t}")
-            first_layer(t, [0, 1], 2 * t, h[:, 0:HALF])
-            first_layer(t, [2], 2 * t + 1, h[:, HALF:S])
-            scatter(up[t], slice(0, S), h[:])
+        for t in (3, 2, 1):
+            quantize_w1(t)
+        h_late.append(keep.tile([P, S], F32, name="h_late", tag="w1_raw1"))
+        first_layer(1, (0, (FIRST, HALF, S)))
+        scatter_on_vector(0, FIRST, S)
+        first_layer(2, (3, (0, FIRST)))
+        scatter_on_scalar(3, 0, FIRST, 3)
+        first_layer(3, (2, (FIRST, HALF, S)))
+        first_layer(4, (2, (0, FIRST)), (3, (FIRST, HALF, S)))
+        scatter_on_vector(2, 0, S)
+        scatter_on_scalar(3, FIRST, S, 3)
+        pre = psum.tile([P, S], F32, name="pre", tag="bank4")
+        nc.tensor.matmul_mx(
+            out=pre[:],
+            lhsT=w1_codes[1][:].bitcast(FP8X4),
+            lhsT_scale=w1_scale[1][:],
+            rhs=x_codes[:].bitcast(FP8X4),
+            rhs_scale=x_scale[:],
+            start=True,
+            stop=True,
+        )
+        nc.scalar.activation(values(1, 0, SHARE), pre[:, 0:SHARE], GELU)
+        nc.scalar.activation(values(1, SHARE, S), pre[:, SHARE:S], GELU)
+        scatter_on_vector(1, SHARE, S)
+        scatter_on_scalar(1, 0, SHARE, PACK)
 
-        blocks = U // 2 // P
-        banked = (0, 1, 4, 5)
-        skip_there = psum.tile([P, blocks, P], F32, name="skip_there", tag="bank2")
-        for n, i in enumerate(banked):
-            nc.tensor.transpose(skip_there[:, n, :], skip_last[:, i * P : (i + 1) * P], identity[:])
-        skip_turned = keep.tile([P, blocks, P], F32, name="skip_turned")
-        nc.scalar.copy(skip_turned[:], skip_there[:])
-        skip_bank = psum.tile([P, blocks * P], F32, name="skip_bank", tag="bank3")
-        for n in range(blocks):
-            nc.tensor.transpose(skip_bank[:, n * P : (n + 1) * P], skip_turned[:, n, :], identity[:])
-        z_turned = [keep.tile([P, U // 2], F32, name=f"z_turned{c}")[:] for c in range(2)]
-        for a in range(2):
-            for c in range(2):
-                turned = psum.tile([P, blocks, P], F32, name="turned", tag=f"bank{4 + 2 * a + c}")
-                sources = ((skip_rows[0], up_first[:], up[0][:]), (skip_rows[1], up[1][:]))[a]
-                for n, source in enumerate(sources):
-                    for b in range(blocks):
-                        first = (c * blocks + b) * P
-                        nc.tensor.matmul(
-                            turned[:, b, :],
-                            source[:, first : first + P],
-                            identity[:],
-                            start=(n == 0 and b == 0),
-                            stop=(n == len(sources) - 1 and b == blocks - 1),
-                            is_transpose=True,
-                        )
-                pairs = z_turned[c].bitcast(BF16).rearrange("p (b m e) -> p b m e", b=blocks, e=2)
-                nc.scalar.copy(
-                    pairs[:, :, a * P // 2 : (a + 1) * P // 2, :],
-                    turned[:].rearrange("p b (e m) -> p b m e", e=2),
-                )
-        for c in range(2):
-            back = psum.tile([P, blocks * P], F32, name="back", tag=f"bank{c}")
-            for b in range(blocks):
-                nc.tensor.transpose(back[:, b * P : (b + 1) * P], z_turned[c][:, b * P : (b + 1) * P], identity[:])
-            nc.scalar.copy(z_pairs[:, c * U // 2 : (c + 1) * U // 2], back[:])
-        woven = z_words[:].rearrange("p (v u) -> p v u", u=2)
-        paired = z_pairs[:].rearrange("p (u v) -> p v u", u=2)
         c = [slice(i, i + CHUNK) for i in range(0, U, CHUNK)]
+        halves = z_pairs[:].bitcast(BF16).rearrange("p (i u v e) -> p i u v e", u=2, v=CHUNK, e=2)
 
-        def pair(i):
-            return slice(c[i].start, c[i + 1].stop)
+        def add_skip(e, chunks):
+            cells = slice(chunks.start * CHUNK, chunks.stop * CHUNK)
+            nc.gpsimd.tensor_tensor(
+                halves[:, chunks, 1, :, e],
+                up[2 + e][:, cells].rearrange("p (i v) -> p i v", v=CHUNK),
+                skip_high[e][:, cells].rearrange("p (i v) -> p i v", v=CHUNK),
+                ADD,
+            )
 
-        skip_end = keep.tile([P, U // 4], F32, name="skip_end", tag="z_turned1")
-        nc.sync.dma_start(out=skip_end[:], in_=skip_planes[:, PACK - 1, pair(6)])
-        for cells in (slice(0, U // 2), slice(U // 2, U)):
-            nc.gpsimd.tensor_tensor(z_high[:, cells, 0], up[2][:, cells], skip_rows[2][:, cells], ADD)
-        for cells in (pair(2), c[0]):
-            nc.scalar.copy(woven[:, cells, :], paired[:, cells, :])
+        add_skip(1, slice(0, 4))
+        add_skip(0, slice(0, 2))
+        add_skip(0, slice(2, 4))
 
+        freed = ("x_codes", "x_scale")
+        z_turned = [keep.tile([P, CHUNK], F32, name=f"z_turned{i}", tag=tag, align_bytes=64)[:] for i, tag in enumerate(freed)]
+        z_turned_late = keep.tile([P, SIDE], F32, name="z_turned_late", tag="h1", align_bytes=64)
+        z_turned = z_turned + [z_turned_late[:, i * CHUNK : (i + 1) * CHUNK] for i in range(2)]
+
+        def turn(turned, sources, cells, first_source, last_source):
+            for n, source in enumerate(sources):
+                for b, first in enumerate(range(cells.start, cells.stop, P)):
+                    nc.tensor.matmul(
+                        turned[:, b, :],
+                        source[:, first : first + P],
+                        identity[:],
+                        start=(first_source and n == 0 and b == 0),
+                        stop=(last_source and n == len(sources) - 1 and first + P == cells.stop),
+                        is_transpose=True,
+                    )
+
+        def round_pairs(copy, a, turned, words):
+            pairs = words.bitcast(BF16).rearrange("p (b m e) -> p b m e", m=P, e=2)
+            copy(pairs[:, :, a * P // 2 : (a + 1) * P // 2, :], turned.rearrange("p b (e m) -> p b m e", e=2))
+
+        for side in range(2):
+            cells = slice(side * SIDE, (side + 1) * SIDE)
+            turned = psum.tile([P, SIDE // P, P], F32, name="turned", tag=f"bank{6 + side}")
+            turn(turned, (skip_low[0], up[0]), cells, True, True)
+            if side == 0:
+                for i in range(2):
+                    round_pairs(on_scalar, 0, turned[:, 2 * i : 2 * i + 2, :], z_turned[i])
+            else:
+                round_pairs(on_vector, 0, turned[:], z_turned_late[:])
+
+        last_banks = (0, 1, 2, 5)
+        turned_last = [psum.tile([P, CHUNK // P, P], F32, name=f"turned_last{i}", tag=f"bank{bank}") for i, bank in enumerate(last_banks)]
+        for i, cells in enumerate(c):
+            turn(turned_last[i], (skip_low[1],), cells, True, False)
+        for i, cells in enumerate(c):
+            turn(turned_last[i], (up[PACK],), cells, False, False)
+
+        z_words = keep.tile([P, 2 * U], F32, name="z_words", align_bytes=64)
         z_codes = keep.tile([P, U], U32, name="z_codes", align_bytes=64)
         z_scale = keep.tile([P, U], U8, name="z_scale", align_bytes=64)
         out_blocks = out.rearrange("(b m) v -> m b v", m=P)
 
-        z_last = z_words[:].bitcast(BF16).rearrange("p (v t) -> p v t", t=PACK)[:, :, PACK - 1]
+        def round_last(copy, i):
+            turn(turned_last[i], (up[1],), c[i], False, True)
+            round_pairs(copy, 1, turned_last[i][:], z_turned[i])
 
-        def add_last(engine, target, cells, addend):
-            engine.tensor_tensor(target[:, cells], up[PACK - 1][:, cells], addend, ADD)
+        def turn_back(copy, i, bank):
+            back = psum.tile([P, CHUNK], F32, name="back", tag=f"bank{bank}")
+            for b in range(CHUNK // P):
+                nc.tensor.transpose(back[:, b * P : (b + 1) * P], z_turned[i][:, b * P : (b + 1) * P], identity[:])
+            copy(z_pairs[:, 2 * c[i].start : 2 * c[i].start + CHUNK], back[:])
 
         def weave(copy, cells):
-            copy(
-                z_words[:].rearrange("p (v u) -> p v u", u=2)[:, cells, :],
-                z_pairs[:].rearrange("p (u v) -> p v u", u=2)[:, cells, :],
-            )
+            words = slice(2 * cells.start, 2 * cells.stop)
+            copy(z_words[:, words].rearrange("p (v u) -> p v u", u=2), z_pairs[:, words].rearrange("p (u v) -> p v u", u=2))
 
         def quantize_z(cells):
             nc.vector.quantize_mx(
@@ -244,56 +280,40 @@ def tile_picked_unet_gelu_e_kernel(tc, xT, w1, w2_words, w2_scales, skip, offs, 
                 in_=z_words[:, 2 * cells.start : 2 * cells.stop].bitcast(BF16),
             )
 
-        def second_layer(acc, b, cells):
-            nc.tensor.matmul_mx(
-                out=acc,
-                lhsT=w2_codes[:, 2 * P * b : 2 * P * (b + 1)].bitcast(FP4X4),
-                lhsT_scale=w2_scale[:, P * b : P * (b + 1)],
-                rhs=z_codes[:, cells].bitcast(FP8X4),
-                rhs_scale=z_scale[:, cells],
-                start=True,
-                stop=True,
-            )
-
         def leave(copy, cells, bank):
             width = cells.stop - cells.start
             acc = psum.tile([P, N // P, width], F32, name="acc", tag=f"bank{bank}")
             for b in range(N // P):
-                second_layer(acc[:, b, :], b, cells)
+                nc.tensor.matmul_mx(
+                    out=acc[:, b, :],
+                    lhsT=w2_codes[:, 2 * P * b : 2 * P * (b + 1)].bitcast(FP4X4),
+                    lhsT_scale=w2_scale[:, P * b : P * (b + 1)],
+                    rhs=z_codes[:, cells].bitcast(FP8X4),
+                    rhs_scale=z_scale[:, cells],
+                    start=True,
+                    stop=True,
+                )
             result = keep.tile([P, N // P, width], F32, name=f"result{cells.start}")
             copy(result[:], acc[:])
             nc.sync.dma_start(out=out_blocks[:, :, cells], in_=result[:])
 
-        def leave_block(copy, cells, b, bank):
-            width = cells.stop - cells.start
-            acc = psum.tile([P, width], F32, name="acc", tag=f"bank{bank}")
-            second_layer(acc[:], b, cells)
-            result = keep.tile([P, width], F32, name=f"result{cells.start}_{b}")
-            copy(result[:], acc[:])
-            nc.sync.dma_start(out=out_blocks[:, b, cells], in_=result[:])
-
-        on_scalar, on_vector = nc.scalar.copy, nc.vector.tensor_copy
-        staged = z_high[:, :, 1]
-
-        add_last(nc.gpsimd, z_last, pair(2), skip_last[:, pair(2)])
-        add_last(nc.vector, z_last, c[0], skip_bank[:, c[0]])
-        add_last(nc.vector, staged, pair(4), skip_bank[:, pair(2)])
-        add_last(nc.vector, staged, c[1], skip_bank[:, c[1]])
-        weave(on_scalar, pair(4))
-        quantize_z(c[0])
-        for b in range(N // P):
-            leave_block(on_scalar, c[0], b, 6 + b)
-        quantize_z(pair(2))
-        for b in range(N // P):
-            leave_block(on_scalar, pair(2), b, b)
-        add_last(nc.vector, staged, pair(6), skip_end[:])
+        round_last(on_scalar, 0)
+        round_last(on_vector, 1)
+        turn_back(on_scalar, 0, 3)
+        round_last(on_scalar, 2)
+        round_last(on_vector, 3)
+        turn_back(on_vector, 1, 4)
+        weave(on_vector, c[0])
+        turn_back(on_scalar, 2, 6)
+        turn_back(on_scalar, 3, 7)
         weave(on_vector, c[1])
-        quantize_z(pair(4))
-        weave(on_vector, pair(6))
+        quantize_z(c[0])
+        leave(on_scalar, c[0], 0)
+        weave(on_scalar, c[2])
         quantize_z(c[1])
-        quantize_z(pair(6))
-        leave_block(on_scalar, pair(4), 0, 4)
-        leave_block(on_vector, pair(4), 1, 5)
-        leave(on_scalar, c[1], 2)
-        leave_block(on_scalar, pair(6), 0, 6)
-        leave_block(on_vector, pair(6), 1, 7)
+        weave(on_vector, c[3])
+        leave(on_scalar, c[1], 1)
+        quantize_z(c[2])
+        leave(on_scalar, c[2], 2)
+        quantize_z(c[3])
+        leave(on_vector, c[3], 5)

@@ -24,7 +24,6 @@ LIST_ROWS = 16
 HALF = S // 2
 FIRST = 128
 SIDE = U // 2
-SHARE = 192
 CHUNK = 256
 
 
@@ -39,9 +38,11 @@ def tile_picked_unet_gelu_e_kernel(tc, xT, w1, w2_words, w2_scales, skip, offs, 
         x_rows = [keep.tile([P, T], F32, name=f"x_rows{j}") for j in range(PACK)]
         w1_raw = [keep.tile([P, PACK, H // 2], F32, name=f"w1_raw{a}") for a in range(2)]
         z_pairs = keep.tile([P, 2 * U], F32, name="z_pairs")
+        high_words = z_pairs[:].rearrange("p (i u v) -> p i u v", u=2, v=CHUNK)[:, :, 1, :]
         skip_low = [keep.tile([P, U], F32, name=f"skip_low{a}") for a in range(2)]
-        skip_high = [keep.tile([P, U], F32, name=f"skip_high{e}") for e in range(2)]
-        up = [keep.tile([P, U], F32, name=f"up{t}") for t in range(PACK + 1)]
+        skip_last = keep.tile([P, U], F32, name="skip_last")
+        skip_high = [high_words, skip_last[:].rearrange("p (i v) -> p i v", v=CHUNK)]
+        up = [keep.tile([P, U], F32, name=f"up{t}") for t in range(PACK)]
         w2_codes = keep.tile([P, 2 * N], U8, name="w2_codes", align_bytes=64)
         w2_scale = keep.tile([P, N], U8, name="w2_scale", align_bytes=64)
 
@@ -73,8 +74,8 @@ def tile_picked_unet_gelu_e_kernel(tc, xT, w1, w2_words, w2_scales, skip, offs, 
                     out=skip_low[a][e * P // 2 : (e + 1) * P // 2, :],
                     in_=skip_planes[a * P // 2 : (a + 1) * P // 2, e, :],
                 )
-        for e in (1, 0):
-            nc.sync.dma_start(out=skip_high[e][:], in_=skip_planes[:, 2 + e, :])
+        for e in range(2):
+            nc.sync.dma_start(out=skip_high[e], in_=skip_planes[:, 2 + e, :].rearrange("p (i v) -> p i v", v=CHUNK))
         nc.sync.dma_start(out=w2_codes[:].bitcast(I32), in_=w2_words[0].bitcast(I32))
         for q in range(4):
             nc.sync.dma_start(
@@ -126,13 +127,10 @@ def tile_picked_unet_gelu_e_kernel(tc, xT, w1, w2_words, w2_scales, skip, offs, 
         on_scalar, on_vector = nc.scalar.copy, nc.vector.tensor_copy
         h = [keep.tile([P, S], F32, name=f"h{t}", align_bytes=64) for t in range(PACK)]
         h_late = []
-        h_share = keep.tile([P, SHARE], F32, name="h_share")
 
         def values(t, first, last):
             if t == 0 and first >= FIRST:
                 return h_late[0][:, first:last]
-            if t == 1 and last <= SHARE:
-                return h_share[:, first:last]
             return h[t][:, first:last]
 
         def first_layer(bank, *parts):
@@ -160,8 +158,8 @@ def tile_picked_unet_gelu_e_kernel(tc, xT, w1, w2_words, w2_scales, skip, offs, 
         def scatter_on_vector(t, first, last):
             nc.vector.tensor_copy(window(t, first, last), values(t, first, last))
 
-        def scatter_on_scalar(t, first, last, w):
-            nc.scalar.activation(window(w, first, last), values(t, first, last), COPY)
+        def scatter_on_scalar(t, first, last):
+            nc.scalar.activation(window(t, first, last), values(t, first, last), COPY)
 
         quantize_x(0, FIRST)
         for rows in row_pairs:
@@ -174,52 +172,40 @@ def tile_picked_unet_gelu_e_kernel(tc, xT, w1, w2_words, w2_scales, skip, offs, 
         scatter_on_vector(0, 0, FIRST)
         group_low(nc.gpsimd.tensor_copy, 1, slice(0, PACK), "p e m j")
         group_high(1)
-        for t in (3, 2, 1):
+        for t in (1, 2, 3):
             quantize_w1(t)
         h_late.append(keep.tile([P, S], F32, name="h_late", tag="w1_raw1"))
         first_layer(1, (0, (FIRST, HALF, S)))
         scatter_on_vector(0, FIRST, S)
-        first_layer(2, (3, (0, FIRST)))
-        scatter_on_scalar(3, 0, FIRST, 3)
+        first_layer(2, (1, (0, FIRST)))
+        scatter_on_scalar(1, 0, FIRST)
         first_layer(3, (2, (FIRST, HALF, S)))
         first_layer(4, (2, (0, FIRST)), (3, (FIRST, HALF, S)))
         scatter_on_vector(2, 0, S)
-        scatter_on_scalar(3, FIRST, S, 3)
-        pre = psum.tile([P, S], F32, name="pre", tag="bank4")
-        nc.tensor.matmul_mx(
-            out=pre[:],
-            lhsT=w1_codes[1][:].bitcast(FP8X4),
-            lhsT_scale=w1_scale[1][:],
-            rhs=x_codes[:].bitcast(FP8X4),
-            rhs_scale=x_scale[:],
-            start=True,
-            stop=True,
-        )
-        nc.scalar.activation(values(1, 0, SHARE), pre[:, 0:SHARE], GELU)
-        nc.scalar.activation(values(1, SHARE, S), pre[:, SHARE:S], GELU)
-        scatter_on_vector(1, SHARE, S)
-        scatter_on_scalar(1, 0, SHARE, PACK)
+        first_layer(5, (3, (0, FIRST)), (1, (FIRST, HALF, S)))
+        scatter_on_scalar(3, HALF, S)
+        scatter_on_scalar(1, FIRST, HALF)
+        scatter_on_scalar(3, 0, HALF)
+        scatter_on_vector(1, HALF, S)
 
         c = [slice(i, i + CHUNK) for i in range(0, U, CHUNK)]
         halves = z_pairs[:].bitcast(BF16).rearrange("p (i u v e) -> p i u v e", u=2, v=CHUNK, e=2)
 
-        def add_skip(e, chunks):
+        def add_skip(engine, e, chunks):
             cells = slice(chunks.start * CHUNK, chunks.stop * CHUNK)
-            nc.gpsimd.tensor_tensor(
+            engine.tensor_tensor(
                 halves[:, chunks, 1, :, e],
                 up[2 + e][:, cells].rearrange("p (i v) -> p i v", v=CHUNK),
-                skip_high[e][:, cells].rearrange("p (i v) -> p i v", v=CHUNK),
+                skip_high[e][:, chunks, :],
                 ADD,
             )
 
-        add_skip(1, slice(0, 4))
-        add_skip(0, slice(0, 2))
-        add_skip(0, slice(2, 4))
+        add_skip(nc.gpsimd, 0, slice(0, 4))
+        add_skip(nc.gpsimd, 1, slice(0, 2))
+        add_skip(nc.gpsimd, 1, slice(2, 4))
 
-        freed = ("x_codes", "x_scale")
-        z_turned = [keep.tile([P, CHUNK], F32, name=f"z_turned{i}", tag=tag, align_bytes=64)[:] for i, tag in enumerate(freed)]
-        z_turned_late = keep.tile([P, SIDE], F32, name="z_turned_late", tag="h1", align_bytes=64)
-        z_turned = z_turned + [z_turned_late[:, i * CHUNK : (i + 1) * CHUNK] for i in range(2)]
+        z_sides = [keep.tile([P, SIDE], F32, name=f"z_side{side}", tag=tag, align_bytes=64) for side, tag in enumerate(("h3", "h1"))]
+        z_turned = [z_sides[i // 2][:, i % 2 * CHUNK : (i % 2 + 1) * CHUNK] for i in range(len(c))]
 
         def turn(turned, sources, cells, first_source, last_source):
             for n, source in enumerate(sources):
@@ -241,18 +227,12 @@ def tile_picked_unet_gelu_e_kernel(tc, xT, w1, w2_words, w2_scales, skip, offs, 
             cells = slice(side * SIDE, (side + 1) * SIDE)
             turned = psum.tile([P, SIDE // P, P], F32, name="turned", tag=f"bank{6 + side}")
             turn(turned, (skip_low[0], up[0]), cells, True, True)
-            if side == 0:
-                for i in range(2):
-                    round_pairs(on_scalar, 0, turned[:, 2 * i : 2 * i + 2, :], z_turned[i])
-            else:
-                round_pairs(on_vector, 0, turned[:], z_turned_late[:])
+            round_pairs((on_scalar, on_vector)[side], 0, turned[:], z_sides[side][:])
 
-        last_banks = (0, 1, 2, 5)
+        last_banks = (0, 1, 2, 3)
         turned_last = [psum.tile([P, CHUNK // P, P], F32, name=f"turned_last{i}", tag=f"bank{bank}") for i, bank in enumerate(last_banks)]
         for i, cells in enumerate(c):
             turn(turned_last[i], (skip_low[1],), cells, True, False)
-        for i, cells in enumerate(c):
-            turn(turned_last[i], (up[PACK],), cells, False, False)
 
         z_words = keep.tile([P, 2 * U], F32, name="z_words", align_bytes=64)
         z_codes = keep.tile([P, U], U32, name="z_codes", align_bytes=64)
@@ -299,21 +279,21 @@ def tile_picked_unet_gelu_e_kernel(tc, xT, w1, w2_words, w2_scales, skip, offs, 
 
         round_last(on_scalar, 0)
         round_last(on_vector, 1)
-        turn_back(on_scalar, 0, 3)
+        turn_back(on_scalar, 0, 4)
         round_last(on_scalar, 2)
         round_last(on_vector, 3)
-        turn_back(on_vector, 1, 4)
-        weave(on_vector, c[0])
-        turn_back(on_scalar, 2, 6)
+        turn_back(on_vector, 1, 5)
+        weave(on_scalar, c[0])
+        turn_back(on_vector, 2, 6)
+        quantize_z(c[0])
         turn_back(on_scalar, 3, 7)
         weave(on_vector, c[1])
-        quantize_z(c[0])
-        leave(on_scalar, c[0], 0)
         weave(on_scalar, c[2])
+        leave(on_scalar, c[0], 0)
         quantize_z(c[1])
         weave(on_vector, c[3])
         leave(on_scalar, c[1], 1)
         quantize_z(c[2])
         leave(on_scalar, c[2], 2)
         quantize_z(c[3])
-        leave(on_vector, c[3], 5)
+        leave(on_vector, c[3], 3)

@@ -183,10 +183,10 @@ def tile_picked_unet_gelu_e_kernel(tc, xT, w1, w2_words, w2_scales, skip, offs, 
         first_layer(4, (2, (0, FIRST)), (3, (FIRST, HALF, S)))
         scatter_on_vector(2, 0, S)
         first_layer(5, (3, (0, FIRST)), (1, (FIRST, HALF, S)))
-        scatter_on_scalar(3, HALF, S)
-        scatter_on_scalar(1, FIRST, HALF)
-        scatter_on_scalar(3, 0, HALF)
-        scatter_on_vector(1, HALF, S)
+        scatter_on_scalar(3, S - FIRST, S)
+        scatter_on_scalar(1, FIRST, S - FIRST)
+        scatter_on_scalar(3, 0, S - FIRST)
+        scatter_on_vector(1, S - FIRST, S)
 
         c = [slice(i, i + CHUNK) for i in range(0, U, CHUNK)]
         halves = z_pairs[:].bitcast(BF16).rearrange("p (i u v e) -> p i u v e", u=2, v=CHUNK, e=2)
@@ -201,10 +201,8 @@ def tile_picked_unet_gelu_e_kernel(tc, xT, w1, w2_words, w2_scales, skip, offs, 
             )
 
         add_skip(nc.gpsimd, 0, slice(0, 4))
-        add_skip(nc.gpsimd, 1, slice(0, 2))
-        add_skip(nc.gpsimd, 1, slice(2, 4))
 
-        z_sides = [keep.tile([P, SIDE], F32, name=f"z_side{side}", tag=tag, align_bytes=64) for side, tag in enumerate(("h3", "h1"))]
+        z_sides = [keep.tile([P, SIDE], F32, name=f"z_side{side}", tag=tag, align_bytes=64) for side, tag in enumerate(("h1", "h3"))]
         z_turned = [z_sides[i // 2][:, i % 2 * CHUNK : (i % 2 + 1) * CHUNK] for i in range(len(c))]
 
         def turn(turned, sources, cells, first_source, last_source):
@@ -227,7 +225,7 @@ def tile_picked_unet_gelu_e_kernel(tc, xT, w1, w2_words, w2_scales, skip, offs, 
             cells = slice(side * SIDE, (side + 1) * SIDE)
             turned = psum.tile([P, SIDE // P, P], F32, name="turned", tag=f"bank{6 + side}")
             turn(turned, (skip_low[0], up[0]), cells, True, True)
-            round_pairs((on_scalar, on_vector)[side], 0, turned[:], z_sides[side][:])
+            round_pairs((on_vector, on_scalar)[side], 0, turned[:], z_sides[side][:])
 
         last_banks = (0, 1, 2, 3)
         turned_last = [psum.tile([P, CHUNK // P, P], F32, name=f"turned_last{i}", tag=f"bank{bank}") for i, bank in enumerate(last_banks)]
@@ -277,23 +275,30 @@ def tile_picked_unet_gelu_e_kernel(tc, xT, w1, w2_words, w2_scales, skip, offs, 
             copy(result[:], acc[:])
             nc.sync.dma_start(out=out_blocks[:, :, cells], in_=result[:])
 
-        round_last(on_scalar, 0)
+        def add_last(i):
+            add_skip(nc.vector, 1, slice(i, i + 1))
+
+        round_last(on_vector, 0)
         round_last(on_vector, 1)
+        add_last(0)
         turn_back(on_scalar, 0, 4)
-        round_last(on_scalar, 2)
-        round_last(on_vector, 3)
-        turn_back(on_vector, 1, 5)
+        add_last(1)
         weave(on_scalar, c[0])
-        turn_back(on_vector, 2, 6)
+        round_last(on_vector, 2)
+        turn_back(on_scalar, 1, 5)
         quantize_z(c[0])
-        turn_back(on_scalar, 3, 7)
-        weave(on_vector, c[1])
-        weave(on_scalar, c[2])
+        round_last(on_vector, 3)
+        weave(on_scalar, c[1])
+        add_last(2)
+        turn_back(on_scalar, 2, 6)
         leave(on_scalar, c[0], 0)
+        add_last(3)
         quantize_z(c[1])
-        weave(on_vector, c[3])
+        turn_back(on_scalar, 3, 7)
+        weave(on_vector, c[2])
         leave(on_scalar, c[1], 1)
+        weave(on_vector, c[3])
         quantize_z(c[2])
-        leave(on_scalar, c[2], 2)
         quantize_z(c[3])
+        leave(on_scalar, c[2], 2)
         leave(on_vector, c[3], 3)

@@ -71,7 +71,7 @@ def tile_picked_unet_gelu_e_kernel(tc, xT, w1, w2_words, w2_scales, skip, offs, 
         for a in range(2):
             for e in range(2):
                 nc.sync.dma_start(
-                    out=skip_low[a][e * P // 2 : (e + 1) * P // 2, :],
+                    out=skip_low[a][e:P:2, :],
                     in_=skip_planes[a * P // 2 : (a + 1) * P // 2, e, :],
                 )
         for e in range(2):
@@ -107,7 +107,7 @@ def tile_picked_unet_gelu_e_kernel(tc, xT, w1, w2_words, w2_scales, skip, offs, 
 
         def group_low(copy, a, rows, order):
             copy(
-                w1_low[a][:].rearrange("p (e m) j -> p e m j", e=2)[:, :, :, rows].rearrange(f"p e m j -> {order}"),
+                w1_low[a][:].rearrange("p (m e) j -> p e m j", e=2)[:, :, :, rows].rearrange(f"p e m j -> {order}"),
                 w1_raw[a][:].rearrange("p j (m t) -> p t m j", t=PACK)[:, 0:2, :, rows].rearrange(f"p e m j -> {order}"),
             )
 
@@ -170,7 +170,7 @@ def tile_picked_unet_gelu_e_kernel(tc, xT, w1, w2_words, w2_scales, skip, offs, 
         group_high(0)
         first_layer(0, (0, (0, FIRST)))
         scatter_on_vector(0, 0, FIRST)
-        group_low(nc.gpsimd.tensor_copy, 1, slice(0, PACK), "p e m j")
+        group_low(nc.gpsimd.tensor_copy, 1, slice(0, PACK), "p m e j")
         group_high(1)
         for t in (1, 2, 3):
             quantize_w1(t)
@@ -218,13 +218,12 @@ def tile_picked_unet_gelu_e_kernel(tc, xT, w1, w2_words, w2_scales, skip, offs, 
                     )
 
         def round_pairs(copy, a, turned, words):
-            pairs = words.bitcast(BF16).rearrange("p (b m e) -> p b m e", m=P, e=2)
-            copy(pairs[:, :, a * P // 2 : (a + 1) * P // 2, :], turned.rearrange("p b (e m) -> p b m e", e=2))
+            copy(words.bitcast(BF16).rearrange("p (b a q) -> p b a q", a=2, q=P)[:, :, a, :], turned)
 
         for side in range(2):
             cells = slice(side * SIDE, (side + 1) * SIDE)
             turned = psum.tile([P, SIDE // P, P], F32, name="turned", tag=f"bank{6 + side}")
-            turn(turned, (skip_low[0], up[0]), cells, True, True)
+            turn(turned, (up[0], skip_low[0]), cells, True, True)
             round_pairs((on_vector, on_scalar)[side], 0, turned[:], z_sides[side][:])
 
         last_banks = (0, 1, 2, 3)

@@ -226,7 +226,7 @@ def tile_picked_unet_gelu_e_kernel(tc, xT, w1, w2_words, w2_scales, skip, offs, 
             turn(turned, (up[0], skip_low[0]), cells, True, True)
             round_pairs((on_vector, on_scalar)[side], 0, turned[:], z_sides[side][:])
 
-        last_banks = (0, 1, 2, 3)
+        last_banks = (3, 4, 5, 2)
         turned_last = [psum.tile([P, CHUNK // P, P], F32, name=f"turned_last{i}", tag=f"bank{bank}") for i, bank in enumerate(last_banks)]
         for i, cells in enumerate(c):
             turn(turned_last[i], (skip_low[1],), cells, True, False)
@@ -280,24 +280,24 @@ def tile_picked_unet_gelu_e_kernel(tc, xT, w1, w2_words, w2_scales, skip, offs, 
         round_last(on_vector, 0)
         round_last(on_vector, 1)
         add_last(0)
-        turn_back(on_scalar, 0, 4)
+        turn_back(on_scalar, 0, 0)
         add_last(1)
         weave(on_scalar, c[0])
         round_last(on_vector, 2)
-        turn_back(on_scalar, 1, 5)
+        turn_back(on_scalar, 1, 1)
         quantize_z(c[0])
         round_last(on_vector, 3)
         weave(on_scalar, c[1])
         add_last(2)
         turn_back(on_scalar, 2, 6)
-        leave(on_scalar, c[0], 0)
+        leave(on_scalar, c[0], 3)
         add_last(3)
         quantize_z(c[1])
         turn_back(on_scalar, 3, 7)
         weave(on_vector, c[2])
-        leave(on_scalar, c[1], 1)
+        leave(on_scalar, c[1], 4)
         weave(on_vector, c[3])
         quantize_z(c[2])
         quantize_z(c[3])
-        leave(on_scalar, c[2], 2)
-        leave(on_vector, c[3], 3)
+        leave(on_scalar, c[2], 5)
+        leave(on_vector, c[3], 2)

@@ -25,6 +25,7 @@ HALF = S // 2
 FIRST = 128
 SIDE = U // 2
 CHUNK = 256
+SHARE = 256
 
 
 def tile_picked_unet_gelu_e_kernel(tc, xT, w1, w2_words, w2_scales, skip, offs, cell, out):
@@ -42,7 +43,7 @@ def tile_picked_unet_gelu_e_kernel(tc, xT, w1, w2_words, w2_scales, skip, offs, 
         skip_low = [keep.tile([P, U], F32, name=f"skip_low{a}") for a in range(2)]
         skip_last = keep.tile([P, U], F32, name="skip_last")
         skip_high = [high_words, skip_last[:].rearrange("p (i v) -> p i v", v=CHUNK)]
-        up = [keep.tile([P, U], F32, name=f"up{t}") for t in range(PACK)]
+        up = [keep.tile([P, U], F32, name=f"up{t}") for t in range(PACK + 1)]
         w2_codes = keep.tile([P, 2 * N], U8, name="w2_codes", align_bytes=64)
         w2_scale = keep.tile([P, N], U8, name="w2_scale", align_bytes=64)
 
@@ -53,6 +54,8 @@ def tile_picked_unet_gelu_e_kernel(tc, xT, w1, w2_words, w2_scales, skip, offs, 
         identity = keep.tile([P, P], F32, name="identity")
         make_identity(nc, identity[:])
 
+        ones = keep.tile([P, 1], F32, name="ones")
+        nc.vector.memset(ones[:], 1.0)
         warm = keep.tile([P, 1], F32, name="warm")
         nc.scalar.activation(warm[:], up[0][:, 0:1], GELU)
 
@@ -111,10 +114,10 @@ def tile_picked_unet_gelu_e_kernel(tc, xT, w1, w2_words, w2_scales, skip, offs, 
                 w1_raw[a][:].rearrange("p j (m t) -> p t m j", t=PACK)[:, 0:2, :, rows].rearrange(f"p e m j -> {order}"),
             )
 
-        def group_high(a):
-            nc.scalar.copy(
-                w1_high[:, :, a * P // 2 : (a + 1) * P // 2, :].rearrange("p t m j -> p m j t"),
-                w1_raw[a][:].rearrange("p j (m t) -> p m j t", t=PACK)[:, :, :, 2:PACK],
+        def group_high(copy, a, order):
+            copy(
+                w1_high[:, :, a * P // 2 : (a + 1) * P // 2, :].rearrange(f"p t m j -> {order}"),
+                w1_raw[a][:].rearrange("p j (m t) -> p t m j", t=PACK)[:, 2:PACK, :, :].rearrange(f"p t m j -> {order}"),
             )
 
         def quantize_w1(t):
@@ -125,7 +128,9 @@ def tile_picked_unet_gelu_e_kernel(tc, xT, w1, w2_words, w2_scales, skip, offs, 
             )
 
         on_scalar, on_vector = nc.scalar.copy, nc.vector.tensor_copy
-        h = [keep.tile([P, S], F32, name=f"h{t}", align_bytes=64) for t in range(PACK)]
+        h = [keep.tile([P, S], F32, name=f"h{t}", align_bytes=64) for t in (0, 2)]
+        h_last = keep.tile([P, 2 * S], F32, name="h_last", align_bytes=64)
+        h = [h[0][:], h_last[:, 0:S], h[1][:], h_last[:, S:]]
         h_late = []
 
         def values(t, first, last):
@@ -133,7 +138,7 @@ def tile_picked_unet_gelu_e_kernel(tc, xT, w1, w2_words, w2_scales, skip, offs, 
                 return h_late[0][:, first:last]
             return h[t][:, first:last]
 
-        def first_layer(bank, *parts):
+        def first_layer(bank, *parts, target=None, pieces=None):
             pre = psum.tile([P, S], F32, name="pre", tag=f"bank{bank}")
             places = []
             for t, cuts in parts:
@@ -149,8 +154,12 @@ def tile_picked_unet_gelu_e_kernel(tc, xT, w1, w2_words, w2_scales, skip, offs, 
                         start=True,
                         stop=True,
                     )
-            for (t, cuts), place in zip(parts, places):
-                nc.scalar.activation(values(t, cuts[0], cuts[-1]), pre[:, place], GELU)
+            if target is None:
+                t, cuts = parts[0]
+                for first, last in pieces or [(cuts[0], cuts[-1])]:
+                    nc.scalar.activation(values(t, first, last), pre[:, first - cuts[0] : last - cuts[0]], GELU)
+            else:
+                nc.scalar.activation(target, pre[:].rearrange("p (a s) -> p a s", a=2), GELU)
 
         def window(t, first, last):
             return up[t][:].indirect(cell_sb[:, first // LIST_ROWS : last // LIST_ROWS])
@@ -167,26 +176,25 @@ def tile_picked_unet_gelu_e_kernel(tc, xT, w1, w2_words, w2_scales, skip, offs, 
         quantize_w1(0)
         quantize_x(FIRST, HALF)
         quantize_x(HALF, S)
-        group_high(0)
+        group_high(on_scalar, 0, "p m j t")
         first_layer(0, (0, (0, FIRST)))
         scatter_on_vector(0, 0, FIRST)
-        group_low(nc.gpsimd.tensor_copy, 1, slice(0, PACK), "p m e j")
-        group_high(1)
+        group_low(on_scalar, 1, slice(0, PACK), "p m j e")
+        group_high(nc.gpsimd.tensor_copy, 1, "p m t j")
         for t in (1, 2, 3):
             quantize_w1(t)
         h_late.append(keep.tile([P, S], F32, name="h_late", tag="w1_raw1"))
-        first_layer(1, (0, (FIRST, HALF, S)))
-        scatter_on_vector(0, FIRST, S)
-        first_layer(2, (1, (0, FIRST)))
-        scatter_on_scalar(1, 0, FIRST)
-        first_layer(3, (2, (FIRST, HALF, S)))
-        first_layer(4, (2, (0, FIRST)), (3, (FIRST, HALF, S)))
+        first_layer(1, (0, (FIRST, HALF, S)), pieces=[(S - FIRST, S), (FIRST, S - FIRST)])
+        scatter_on_vector(0, FIRST, S - FIRST)
+        nc.scalar.activation(up[PACK][:].indirect(cell_sb[:, (S - FIRST) // LIST_ROWS :]), values(0, S - FIRST, S), COPY)
+        first_layer(2, (2, (0, S)))
+        quarters = h_last[:].rearrange("p (a s) -> p a s", s=HALF)
+        first_layer(1, (1, (0, HALF)), (3, (HALF, S)), target=quarters[:, 0:4:3, :])
+        first_layer(3, (1, (HALF, S)), (3, (0, HALF)), target=quarters[:, 1:3, :])
         scatter_on_vector(2, 0, S)
-        first_layer(5, (3, (0, FIRST)), (1, (FIRST, HALF, S)))
-        scatter_on_scalar(3, S - FIRST, S)
-        scatter_on_scalar(1, FIRST, S - FIRST)
-        scatter_on_scalar(3, 0, S - FIRST)
-        scatter_on_vector(1, S - FIRST, S)
+        scatter_on_scalar(1, 0, SHARE)
+        nc.scalar.activation(window(3, 0, S), values(3, 0, S), COPY, scale=ones[:])
+        scatter_on_vector(1, SHARE, S)
 
         c = [slice(i, i + CHUNK) for i in range(0, U, CHUNK)]
         halves = z_pairs[:].bitcast(BF16).rearrange("p (i u v e) -> p i u v e", u=2, v=CHUNK, e=2)
@@ -202,7 +210,7 @@ def tile_picked_unet_gelu_e_kernel(tc, xT, w1, w2_words, w2_scales, skip, offs, 
 
         add_skip(nc.gpsimd, 0, slice(0, 4))
 
-        z_sides = [keep.tile([P, SIDE], F32, name=f"z_side{side}", tag=tag, align_bytes=64) for side, tag in enumerate(("h1", "h3"))]
+        z_sides = [h_last[:, side * SIDE : (side + 1) * SIDE] for side in range(2)]
         z_turned = [z_sides[i // 2][:, i % 2 * CHUNK : (i % 2 + 1) * CHUNK] for i in range(len(c))]
 
         def turn(turned, sources, cells, first_source, last_source):
@@ -223,8 +231,8 @@ def tile_picked_unet_gelu_e_kernel(tc, xT, w1, w2_words, w2_scales, skip, offs, 
         for side in range(2):
             cells = slice(side * SIDE, (side + 1) * SIDE)
             turned = psum.tile([P, SIDE // P, P], F32, name="turned", tag=f"bank{6 + side}")
-            turn(turned, (up[0], skip_low[0]), cells, True, True)
-            round_pairs((on_vector, on_scalar)[side], 0, turned[:], z_sides[side][:])
+            turn(turned, (up[PACK], up[0], skip_low[0]), cells, True, True)
+            round_pairs((on_vector, on_scalar)[side], 0, turned[:], z_sides[side])
 
         last_banks = (3, 4, 5, 2)
         turned_last = [psum.tile([P, CHUNK // P, P], F32, name=f"turned_last{i}", tag=f"bank{bank}") for i, bank in enumerate(last_banks)]

@@ -209,6 +209,7 @@ def tile_picked_unet_gelu_e_kernel(tc, xT, w1, w2_words, w2_scales, skip, offs, 
             )
 
         add_skip(nc.gpsimd, 0, slice(0, 4))
+        add_skip(nc.gpsimd, 1, slice(1, 2))
 
         z_sides = [h_last[:, side * SIDE : (side + 1) * SIDE] for side in range(2)]
         z_turned = [z_sides[i // 2][:, i % 2 * CHUNK : (i % 2 + 1) * CHUNK] for i in range(len(c))]
@@ -265,12 +266,13 @@ def tile_picked_unet_gelu_e_kernel(tc, xT, w1, w2_words, w2_scales, skip, offs, 
                 in_=z_words[:, 2 * cells.start : 2 * cells.stop].bitcast(BF16),
             )
 
-        def leave(copy, cells, bank):
+        def leave(copies, cells, banks):
             width = cells.stop - cells.start
-            acc = psum.tile([P, N // P, width], F32, name="acc", tag=f"bank{bank}")
-            for b in range(N // P):
+            result = keep.tile([P, N // P, width], F32, name=f"result{cells.start}")
+            for b, (copy, bank) in enumerate(zip(copies, banks)):
+                acc = psum.tile([P, width], F32, name="acc", tag=f"bank{bank}")
                 nc.tensor.matmul_mx(
-                    out=acc[:, b, :],
+                    out=acc[:],
                     lhsT=w2_codes[:, 2 * P * b : 2 * P * (b + 1)].bitcast(FP4X4),
                     lhsT_scale=w2_scale[:, P * b : P * (b + 1)],
                     rhs=z_codes[:, cells].bitcast(FP8X4),
@@ -278,8 +280,7 @@ def tile_picked_unet_gelu_e_kernel(tc, xT, w1, w2_words, w2_scales, skip, offs, 
                     start=True,
                     stop=True,
                 )
-            result = keep.tile([P, N // P, width], F32, name=f"result{cells.start}")
-            copy(result[:], acc[:])
+                copy(result[:, b, :], acc[:])
             nc.sync.dma_start(out=out_blocks[:, :, cells], in_=result[:])
 
         def add_last(i):
@@ -289,23 +290,22 @@ def tile_picked_unet_gelu_e_kernel(tc, xT, w1, w2_words, w2_scales, skip, offs, 
         round_last(on_vector, 1)
         add_last(0)
         turn_back(on_scalar, 0, 0)
-        add_last(1)
         weave(on_scalar, c[0])
         round_last(on_vector, 2)
         turn_back(on_scalar, 1, 1)
         quantize_z(c[0])
         round_last(on_vector, 3)
-        weave(on_scalar, c[1])
+        weave(on_vector, c[1])
         add_last(2)
         turn_back(on_scalar, 2, 6)
-        leave(on_scalar, c[0], 3)
+        leave((on_scalar, on_scalar), c[0], (3, 4))
         add_last(3)
         quantize_z(c[1])
         turn_back(on_scalar, 3, 7)
         weave(on_vector, c[2])
-        leave(on_scalar, c[1], 4)
+        leave((on_scalar, on_scalar), c[1], (5, 2))
         weave(on_vector, c[3])
         quantize_z(c[2])
         quantize_z(c[3])
-        leave(on_scalar, c[2], 5)
-        leave(on_vector, c[3], 2)
+        leave((on_vector, on_scalar), c[2], (0, 1))
+        leave((on_vector, on_scalar), c[3], (6, 7))

@@ -209,7 +209,6 @@ def tile_picked_unet_gelu_e_kernel(tc, xT, w1, w2_words, w2_scales, skip, offs, 
             )
 
         add_skip(nc.gpsimd, 0, slice(0, 4))
-        add_skip(nc.gpsimd, 1, slice(1, 2))
 
         z_sides = [h_last[:, side * SIDE : (side + 1) * SIDE] for side in range(2)]
         z_turned = [z_sides[i // 2][:, i % 2 * CHUNK : (i % 2 + 1) * CHUNK] for i in range(len(c))]
@@ -290,12 +289,13 @@ def tile_picked_unet_gelu_e_kernel(tc, xT, w1, w2_words, w2_scales, skip, offs, 
         round_last(on_vector, 1)
         add_last(0)
         turn_back(on_scalar, 0, 0)
+        add_last(1)
         weave(on_scalar, c[0])
         round_last(on_vector, 2)
         turn_back(on_scalar, 1, 1)
         quantize_z(c[0])
         round_last(on_vector, 3)
-        weave(on_vector, c[1])
+        weave(on_scalar, c[1])
         add_last(2)
         turn_back(on_scalar, 2, 6)
         leave((on_scalar, on_scalar), c[0], (3, 4))

@@ -69,8 +69,8 @@ def tile_picked_unet_gelu_e_kernel(tc, xT, w1, w2_words, w2_scales, skip, offs, 
         row_pairs = (slice(0, 2), slice(2, PACK))
         for rows in row_pairs:
             nc.sync.dma_start(out=w1_raw[0][:, rows, :], in_=w1_planes[:, rows, 0 : H // 2])
-        nc.sync.dma_start(cell_sb[:], cell)
         nc.sync.dma_start(out=w1_raw[1][:], in_=w1_planes[:, :, H // 2 : H])
+        nc.sync.dma_start(cell_sb[:], cell)
         for a in range(2):
             for e in range(2):
                 nc.sync.dma_start(
@@ -86,20 +86,21 @@ def tile_picked_unet_gelu_e_kernel(tc, xT, w1, w2_words, w2_scales, skip, offs, 
                 in_=w2_scales[0, 4 * q : 4 * q + 4, :].bitcast(I32),
             )
 
-        x_grouped = keep.tile([P, S, PACK], BF16, name="x_grouped", align_bytes=64)
+        x_grouped = keep.tile([P, S - FIRST, PACK], BF16, name="x_grouped", align_bytes=64)
+        x_tail = keep.tile([P, FIRST, PACK], BF16, name="x_tail", align_bytes=64)
         x_codes = keep.tile([P, S], U32, name="x_codes", align_bytes=64)
         x_scale = keep.tile([P, S], U8, name="x_scale", align_bytes=64)
-        for j in range(PACK - 1):
-            nc.vector.tensor_copy(x_grouped[:, :, j], x_rows[j][:].indirect(offs_sb[:]))
-        for first in (0, HALF):
-            cols = slice(first // LIST_ROWS, (first + HALF) // LIST_ROWS)
-            nc.vector.tensor_copy(x_grouped[:, first : first + HALF, PACK - 1], x_rows[PACK - 1][:].indirect(offs_sb[:, cols]))
+        cut = (S - FIRST) // LIST_ROWS
+        for j in range(PACK):
+            nc.vector.tensor_copy(x_grouped[:, :, j], x_rows[j][:].indirect(offs_sb[:, 0:cut]))
+            nc.scalar.activation(x_tail[:, :, j], x_rows[j][:].indirect(offs_sb[:, cut:]), COPY)
 
         def quantize_x(first, last):
+            grouped = x_grouped[:, first:last, :] if last <= S - FIRST else x_tail[:]
             nc.vector.quantize_mx(
                 out=x_codes[:, first:last].bitcast(FP8X4),
                 scales=x_scale[:, first:last],
-                in_=x_grouped[:, first:last, :].rearrange("p s j -> p (s j)"),
+                in_=grouped.rearrange("p s j -> p (s j)"),
             )
 
         w1_low = [keep.tile([P, P, PACK], BF16, name=f"w1_low{a}", align_bytes=64) for a in range(2)]
@@ -170,12 +171,12 @@ def tile_picked_unet_gelu_e_kernel(tc, xT, w1, w2_words, w2_scales, skip, offs, 
         def scatter_on_scalar(t, first, last):
             nc.scalar.activation(window(t, first, last), values(t, first, last), COPY)
 
+        quantize_x(S - FIRST, S)
         quantize_x(0, FIRST)
         for rows in row_pairs:
             group_low(on_scalar, 0, rows, "p m j e")
         quantize_w1(0)
-        quantize_x(FIRST, HALF)
-        quantize_x(HALF, S)
+        quantize_x(FIRST, S - FIRST)
         group_high(on_scalar, 0, "p m j t")
         first_layer(0, (0, (0, FIRST)))
         scatter_on_vector(0, 0, FIRST)
@@ -184,7 +185,7 @@ def tile_picked_unet_gelu_e_kernel(tc, xT, w1, w2_words, w2_scales, skip, offs, 
         for t in (1, 2, 3):
             quantize_w1(t)
         h_late.append(keep.tile([P, S], F32, name="h_late", tag="w1_raw1"))
-        first_layer(1, (0, (FIRST, HALF, S)), pieces=[(S - FIRST, S), (FIRST, S - FIRST)])
+        first_layer(1, (0, (FIRST, S - FIRST, S)), pieces=[(S - FIRST, S), (FIRST, S - FIRST)])
         scatter_on_vector(0, FIRST, S - FIRST)
         nc.scalar.activation(up[PACK][:].indirect(cell_sb[:, (S - FIRST) // LIST_ROWS :]), values(0, S - FIRST, S), COPY)
         first_layer(2, (2, (0, S)))

@@ -44,7 +44,6 @@ def tile_picked_unet_gelu_e_kernel(tc, xT, w1, w2_words, w2_scales, skip, offs, 
         skip_last = keep.tile([P, U], F32, name="skip_last")
         skip_high = [high_words, skip_last[:].rearrange("p (i v) -> p i v", v=CHUNK)]
         up = [keep.tile([P, U], F32, name=f"up{t}") for t in range(PACK + 1)]
-        w2_codes = keep.tile([P, 2 * N], U8, name="w2_codes", align_bytes=64)
         w2_scale = keep.tile([P, N], U8, name="w2_scale", align_bytes=64)
 
         nc.vector.memset(w2_scale[:].bitcast(I32), 0)
@@ -79,7 +78,6 @@ def tile_picked_unet_gelu_e_kernel(tc, xT, w1, w2_words, w2_scales, skip, offs, 
                 )
         for e in range(2):
             nc.sync.dma_start(out=skip_high[e], in_=skip_planes[:, 2 + e, :].rearrange("p (i v) -> p i v", v=CHUNK))
-        nc.sync.dma_start(out=w2_codes[:].bitcast(I32), in_=w2_words[0].bitcast(I32))
         for q in range(4):
             nc.sync.dma_start(
                 out=w2_scale[32 * q : 32 * q + 4, :].bitcast(I32),
@@ -178,6 +176,8 @@ def tile_picked_unet_gelu_e_kernel(tc, xT, w1, w2_words, w2_scales, skip, offs, 
         quantize_w1(0)
         quantize_x(FIRST, S - FIRST)
         group_high(on_scalar, 0, "p m j t")
+        w2_codes = keep.tile([P, 2 * N], U8, name="w2_codes", tag="w1_low0", align_bytes=64)
+        nc.scalar.dma_start(out=w2_codes[:].bitcast(I32), in_=w2_words[0].bitcast(I32))
         first_layer(0, (0, (0, FIRST)))
         scatter_on_vector(0, 0, FIRST)
         group_low(on_scalar, 1, slice(0, PACK), "p m j e")
@@ -266,7 +266,7 @@ def tile_picked_unet_gelu_e_kernel(tc, xT, w1, w2_words, w2_scales, skip, offs, 
                 in_=z_words[:, 2 * cells.start : 2 * cells.stop].bitcast(BF16),
             )
 
-        def leave(copies, cells, banks):
+        def leave(copies, cells, banks, queue=nc.sync):
             width = cells.stop - cells.start
             result = keep.tile([P, N // P, width], F32, name=f"result{cells.start}")
             for b, (copy, bank) in enumerate(zip(copies, banks)):
@@ -281,7 +281,7 @@ def tile_picked_unet_gelu_e_kernel(tc, xT, w1, w2_words, w2_scales, skip, offs, 
                     stop=True,
                 )
                 copy(result[:, b, :], acc[:])
-            nc.sync.dma_start(out=out_blocks[:, :, cells], in_=result[:])
+            queue.dma_start(out=out_blocks[:, :, cells], in_=result[:])
 
         def add_last(i):
             add_skip(nc.vector, 1, slice(i, i + 1))
@@ -309,4 +309,4 @@ def tile_picked_unet_gelu_e_kernel(tc, xT, w1, w2_words, w2_scales, skip, offs, 
         quantize_z(c[2])
         quantize_z(c[3])
         leave((on_vector, on_scalar), c[2], (0, 1))
-        leave((on_vector, on_scalar), c[3], (6, 7))
+        leave((on_vector, on_scalar), c[3], (6, 7), nc.scalar)

from contextlib import ExitStack

import concourse.mybir as mybir
from concourse.masks import make_identity

K, T, S, H, N, U = 512, 2048, 512, 512, 256, 1024
FLOPS = 2 * K * H * S + 2 * H * N * U

F32 = mybir.dt.float32
BF16 = mybir.dt.bfloat16
I32 = mybir.dt.int32
U32 = mybir.dt.uint32
U16 = mybir.dt.uint16
U8 = mybir.dt.uint8
FP8X4 = mybir.dt.float8_e4m3fn_x4
FP4X4 = mybir.dt.float4_e2m1fn_x4
ADD = mybir.AluOpType.add
GELU = mybir.ActivationFunctionType.Gelu_apprx_tanh
COPY = mybir.ActivationFunctionType.Copy

P = 128
PACK = 4
LIST_ROWS = 16
HALF = S // 2
FIRST = 128
SIDE = U // 2
CHUNK = 256
SHARE = 256


def tile_picked_unet_gelu_e_kernel(tc, xT, w1, w2_words, w2_scales, skip, offs, cell, out):
    nc = tc.nc
    with ExitStack() as ctx:
        keep = ctx.enter_context(tc.tile_pool(name="keep", bufs=1))
        psum = ctx.enter_context(tc.psum_pool(name="psum", bufs=1))

        offs_sb = keep.tile([P, S // LIST_ROWS], U16, name="offs_sb")
        cell_sb = keep.tile([P, S // LIST_ROWS], U16, name="cell_sb")
        x_rows = [keep.tile([P, T], F32, name=f"x_rows{j}") for j in range(PACK)]
        w1_raw = [keep.tile([P, PACK, H // 2], F32, name=f"w1_raw{a}") for a in range(2)]
        z_pairs = keep.tile([P, 2 * U], F32, name="z_pairs")
        high_words = z_pairs[:].rearrange("p (i u v) -> p i u v", u=2, v=CHUNK)[:, :, 1, :]
        skip_low = [keep.tile([P, U], F32, name=f"skip_low{a}") for a in range(2)]
        skip_last = keep.tile([P, U], F32, name="skip_last")
        skip_high = [high_words, skip_last[:].rearrange("p (i v) -> p i v", v=CHUNK)]
        up = [keep.tile([P, U], F32, name=f"up{t}") for t in range(PACK + 1)]
        w2_scale = keep.tile([P, N], U8, name="w2_scale", align_bytes=64)

        nc.vector.memset(w2_scale[:].bitcast(I32), 0)
        for window in up:
            nc.vector.memset(window[:], 0.0)

        identity = keep.tile([P, P], F32, name="identity")
        make_identity(nc, identity[:])

        ones = keep.tile([P, 1], F32, name="ones")
        nc.vector.memset(ones[:], 1.0)
        warm = keep.tile([P, 1], F32, name="warm")
        nc.scalar.activation(warm[:], up[0][:, 0:1], GELU)

        x_planes = xT.rearrange("(p j) c -> p j c", j=PACK)
        skip_planes = skip.rearrange("(p t) v -> p t v", t=PACK)
        w1_planes = w1.rearrange("(p j) c -> p j c", j=PACK)
        for j in range(PACK):
            nc.sync.dma_start(out=x_rows[j][:], in_=x_planes[:, j, :])
            if j == 0:
                nc.sync.dma_start(offs_sb[:], offs)
        row_pairs = (slice(0, 2), slice(2, PACK))
        for rows in row_pairs:
            nc.sync.dma_start(out=w1_raw[0][:, rows, :], in_=w1_planes[:, rows, 0 : H // 2])
        nc.sync.dma_start(out=w1_raw[1][:], in_=w1_planes[:, :, H // 2 : H])
        nc.sync.dma_start(cell_sb[:], cell)
        for a in range(2):
            for e in range(2):
                nc.sync.dma_start(
                    out=skip_low[a][e:P:2, :],
                    in_=skip_planes[a * P // 2 : (a + 1) * P // 2, e, :],
                )
        for e in range(2):
            nc.sync.dma_start(out=skip_high[e], in_=skip_planes[:, 2 + e, :].rearrange("p (i v) -> p i v", v=CHUNK))
        for q in range(4):
            nc.sync.dma_start(
                out=w2_scale[32 * q : 32 * q + 4, :].bitcast(I32),
                in_=w2_scales[0, 4 * q : 4 * q + 4, :].bitcast(I32),
            )

        x_grouped = keep.tile([P, S - FIRST, PACK], BF16, name="x_grouped", align_bytes=64)
        x_tail = keep.tile([P, FIRST, PACK], BF16, name="x_tail", align_bytes=64)
        x_codes = keep.tile([P, S], U32, name="x_codes", align_bytes=64)
        x_scale = keep.tile([P, S], U8, name="x_scale", align_bytes=64)
        cut = (S - FIRST) // LIST_ROWS
        for j in range(PACK):
            nc.vector.tensor_copy(x_grouped[:, :, j], x_rows[j][:].indirect(offs_sb[:, 0:cut]))
            nc.scalar.activation(x_tail[:, :, j], x_rows[j][:].indirect(offs_sb[:, cut:]), COPY)

        def quantize_x(first, last):
            grouped = x_grouped[:, first:last, :] if last <= S - FIRST else x_tail[:]
            nc.vector.quantize_mx(
                out=x_codes[:, first:last].bitcast(FP8X4),
                scales=x_scale[:, first:last],
                in_=grouped.rearrange("p s j -> p (s j)"),
            )

        w1_low = [keep.tile([P, P, PACK], BF16, name=f"w1_low{a}", align_bytes=64) for a in range(2)]
        w1_high = keep.tile([P, 2, P, PACK], BF16, name="w1_high", align_bytes=64)
        w1_grouped = [w1_low[0][:], w1_low[1][:], w1_high[:, 0, :, :], w1_high[:, 1, :, :]]
        w1_codes = [keep.tile([P, P], U32, name=f"w1_codes{t}", align_bytes=64) for t in range(PACK)]
        w1_scale = [keep.tile([P, P], U8, name=f"w1_scale{t}", align_bytes=64) for t in range(PACK)]

        def group_low(copy, a, rows, order):
            copy(
                w1_low[a][:].rearrange("p (m e) j -> p e m j", e=2)[:, :, :, rows].rearrange(f"p e m j -> {order}"),
                w1_raw[a][:].rearrange("p j (m t) -> p t m j", t=PACK)[:, 0:2, :, rows].rearrange(f"p e m j -> {order}"),
            )

        def group_high(copy, a, order):
            copy(
                w1_high[:, :, a * P // 2 : (a + 1) * P // 2, :].rearrange(f"p t m j -> {order}"),
                w1_raw[a][:].rearrange("p j (m t) -> p t m j", t=PACK)[:, 2:PACK, :, :].rearrange(f"p t m j -> {order}"),
            )

        def quantize_w1(t):
            nc.vector.quantize_mx(
                out=w1_codes[t][:].bitcast(FP8X4),
                scales=w1_scale[t][:],
                in_=w1_grouped[t].rearrange("p m j -> p (m j)"),
            )

        on_scalar, on_vector = nc.scalar.copy, nc.vector.tensor_copy
        h = [keep.tile([P, S], F32, name=f"h{t}", align_bytes=64) for t in (0, 2)]
        h_last = keep.tile([P, 2 * S], F32, name="h_last", align_bytes=64)
        h = [h[0][:], h_last[:, 0:S], h[1][:], h_last[:, S:]]
        h_late = []

        def values(t, first, last):
            if t == 0 and first >= FIRST:
                return h_late[0][:, first:last]
            return h[t][:, first:last]

        def first_layer(bank, *parts, target=None, pieces=None):
            pre = psum.tile([P, S], F32, name="pre", tag=f"bank{bank}")
            places = []
            for t, cuts in parts:
                place = places[-1].stop if places else 0
                places.append(slice(place, place + cuts[-1] - cuts[0]))
                for first, last in zip(cuts, cuts[1:]):
                    nc.tensor.matmul_mx(
                        out=pre[:, place + first - cuts[0] : place + last - cuts[0]],
                        lhsT=w1_codes[t][:].bitcast(FP8X4),
                        lhsT_scale=w1_scale[t][:],
                        rhs=x_codes[:, first:last].bitcast(FP8X4),
                        rhs_scale=x_scale[:, first:last],
                        start=True,
                        stop=True,
                    )
            if target is None:
                t, cuts = parts[0]
                for first, last in pieces or [(cuts[0], cuts[-1])]:
                    nc.scalar.activation(values(t, first, last), pre[:, first - cuts[0] : last - cuts[0]], GELU)
            else:
                nc.scalar.activation(target, pre[:].rearrange("p (a s) -> p a s", a=2), GELU)

        def window(t, first, last):
            return up[t][:].indirect(cell_sb[:, first // LIST_ROWS : last // LIST_ROWS])

        def scatter_on_vector(t, first, last):
            nc.vector.tensor_copy(window(t, first, last), values(t, first, last))

        def scatter_on_scalar(t, first, last):
            nc.scalar.activation(window(t, first, last), values(t, first, last), COPY)

        quantize_x(S - FIRST, S)
        quantize_x(0, FIRST)
        for rows in row_pairs:
            group_low(on_scalar, 0, rows, "p m j e")
        quantize_w1(0)
        quantize_x(FIRST, S - FIRST)
        group_high(on_scalar, 0, "p m j t")
        w2_codes = keep.tile([P, 2 * N], U8, name="w2_codes", tag="w1_low0", align_bytes=64)
        nc.scalar.dma_start(out=w2_codes[:].bitcast(I32), in_=w2_words[0].bitcast(I32))
        first_layer(0, (0, (0, FIRST)))
        scatter_on_vector(0, 0, FIRST)
        group_low(on_scalar, 1, slice(0, PACK), "p m j e")
        group_high(nc.gpsimd.tensor_copy, 1, "p m t j")
        for t in (1, 2, 3):
            quantize_w1(t)
        h_late.append(keep.tile([P, S], F32, name="h_late", tag="w1_raw1"))
        first_layer(1, (0, (FIRST, S - FIRST, S)), pieces=[(S - FIRST, S), (FIRST, S - FIRST)])
        scatter_on_vector(0, FIRST, S - FIRST)
        nc.scalar.activation(up[PACK][:].indirect(cell_sb[:, (S - FIRST) // LIST_ROWS :]), values(0, S - FIRST, S), COPY)
        first_layer(2, (2, (0, S)))
        quarters = h_last[:].rearrange("p (a s) -> p a s", s=HALF)
        first_layer(1, (1, (0, HALF)), (3, (HALF, S)), target=quarters[:, 0:4:3, :])
        first_layer(3, (1, (HALF, S)), (3, (0, HALF)), target=quarters[:, 1:3, :])
        scatter_on_vector(2, 0, S)
        scatter_on_scalar(1, 0, SHARE)
        nc.scalar.activation(window(3, 0, S), values(3, 0, S), COPY, scale=ones[:])
        scatter_on_vector(1, SHARE, S)

        c = [slice(i, i + CHUNK) for i in range(0, U, CHUNK)]
        halves = z_pairs[:].bitcast(BF16).rearrange("p (i u v e) -> p i u v e", u=2, v=CHUNK, e=2)

        def add_skip(engine, e, chunks):
            cells = slice(chunks.start * CHUNK, chunks.stop * CHUNK)
            engine.tensor_tensor(
                halves[:, chunks, 1, :, e],
                up[2 + e][:, cells].rearrange("p (i v) -> p i v", v=CHUNK),
                skip_high[e][:, chunks, :],
                ADD,
            )

        add_skip(nc.gpsimd, 0, slice(0, 4))

        z_sides = [h_last[:, side * SIDE : (side + 1) * SIDE] for side in range(2)]
        z_turned = [z_sides[i // 2][:, i % 2 * CHUNK : (i % 2 + 1) * CHUNK] for i in range(len(c))]

        def turn(turned, sources, cells, first_source, last_source):
            for n, source in enumerate(sources):
                for b, first in enumerate(range(cells.start, cells.stop, P)):
                    nc.tensor.matmul(
                        turned[:, b, :],
                        source[:, first : first + P],
                        identity[:],
                        start=(first_source and n == 0 and b == 0),
                        stop=(last_source and n == len(sources) - 1 and first + P == cells.stop),
                        is_transpose=True,
                    )

        def round_pairs(copy, a, turned, words):
            copy(words.bitcast(BF16).rearrange("p (b a q) -> p b a q", a=2, q=P)[:, :, a, :], turned)

        for side in range(2):
            cells = slice(side * SIDE, (side + 1) * SIDE)
            turned = psum.tile([P, SIDE // P, P], F32, name="turned", tag=f"bank{6 + side}")
            turn(turned, (up[PACK], up[0], skip_low[0]), cells, True, True)
            round_pairs((on_vector, on_scalar)[side], 0, turned[:], z_sides[side])

        last_banks = (3, 4, 5, 2)
        turned_last = [psum.tile([P, CHUNK // P, P], F32, name=f"turned_last{i}", tag=f"bank{bank}") for i, bank in enumerate(last_banks)]
        for i, cells in enumerate(c):
            turn(turned_last[i], (skip_low[1],), cells, True, False)

        z_words = keep.tile([P, 2 * U], F32, name="z_words", align_bytes=64)
        z_codes = keep.tile([P, U], U32, name="z_codes", align_bytes=64)
        z_scale = keep.tile([P, U], U8, name="z_scale", align_bytes=64)
        out_blocks = out.rearrange("(b m) v -> m b v", m=P)

        def round_last(copy, i):
            turn(turned_last[i], (up[1],), c[i], False, True)
            round_pairs(copy, 1, turned_last[i][:], z_turned[i])

        def turn_back(copy, i, bank):
            back = psum.tile([P, CHUNK], F32, name="back", tag=f"bank{bank}")
            for b in range(CHUNK // P):
                nc.tensor.transpose(back[:, b * P : (b + 1) * P], z_turned[i][:, b * P : (b + 1) * P], identity[:])
            copy(z_pairs[:, 2 * c[i].start : 2 * c[i].start + CHUNK], back[:])

        def weave(copy, cells):
            words = slice(2 * cells.start, 2 * cells.stop)
            copy(z_words[:, words].rearrange("p (v u) -> p v u", u=2), z_pairs[:, words].rearrange("p (u v) -> p v u", u=2))

        def quantize_z(cells):
            nc.vector.quantize_mx(
                out=z_codes[:, cells].bitcast(FP8X4),
                scales=z_scale[:, cells],
                in_=z_words[:, 2 * cells.start : 2 * cells.stop].bitcast(BF16),
            )

        def leave(copies, cells, banks, queue=nc.sync):
            width = cells.stop - cells.start
            result = keep.tile([P, N // P, width], F32, name=f"result{cells.start}")
            for b, (copy, bank) in enumerate(zip(copies, banks)):
                acc = psum.tile([P, width], F32, name="acc", tag=f"bank{bank}")
                nc.tensor.matmul_mx(
                    out=acc[:],
                    lhsT=w2_codes[:, 2 * P * b : 2 * P * (b + 1)].bitcast(FP4X4),
                    lhsT_scale=w2_scale[:, P * b : P * (b + 1)],
                    rhs=z_codes[:, cells].bitcast(FP8X4),
                    rhs_scale=z_scale[:, cells],
                    start=True,
                    stop=True,
                )
                copy(result[:, b, :], acc[:])
            queue.dma_start(out=out_blocks[:, :, cells], in_=result[:])

        def add_last(i):
            add_skip(nc.vector, 1, slice(i, i + 1))

        round_last(on_vector, 0)
        round_last(on_vector, 1)
        add_last(0)
        turn_back(on_scalar, 0, 0)
        add_last(1)
        weave(on_scalar, c[0])
        round_last(on_vector, 2)
        turn_back(on_scalar, 1, 1)
        quantize_z(c[0])
        round_last(on_vector, 3)
        weave(on_scalar, c[1])
        add_last(2)
        turn_back(on_scalar, 2, 6)
        leave((on_scalar, on_scalar), c[0], (3, 4))
        add_last(3)
        quantize_z(c[1])
        turn_back(on_scalar, 3, 7)
        weave(on_vector, c[2])
        leave((on_scalar, on_scalar), c[1], (5, 2))
        weave(on_vector, c[3])
        quantize_z(c[2])
        quantize_z(c[3])
        leave((on_vector, on_scalar), c[2], (0, 1))
        leave((on_vector, on_scalar), c[3], (6, 7), nc.scalar)
